import numpy as np, ml_dtypes
CORES = [36,164,52,180,100,228,116,244]
N = 8
import mx_ref
BF = ml_dtypes.bfloat16
def entries(a):
    return np.ascontiguousarray(a.T).reshape(-1)
def table(e):
    return np.ascontiguousarray(np.reshape(e, (-1, 16)).T).astype(np.int32)
def gcols(t, e):
    v = np.concatenate([t.reshape(8, 16, -1, 4), np.zeros((8, 16, 1, 4), BF)], axis=2)
    return np.ascontiguousarray(np.stack([v[g][:, e[g]] for g in range(8)])).reshape(128, -1)
def tile(rs):
    return np.stack(rs, axis=2).reshape(128, -1).astype(BF)
def pick(q, e):
    c = np.concatenate([q[0].reshape(128, -1, 4), np.zeros((128, 1, 4), np.uint8)], axis=1); s = np.concatenate([q[1], np.ones((16, 1), np.uint8)], axis=1)
    return (np.ascontiguousarray(c[:, e].reshape(128, -1)), np.ascontiguousarray(s[:, e]))
def join(*qs):
    return (np.concatenate([q[0] for q in qs], axis=1), np.concatenate([q[1] for q in qs], axis=1))
def put(q, e, v):
    c, s = q[0].reshape(128, -1, 4).copy(), q[1].copy(); c[:, e] = v[0].reshape(128, -1, 4); s[:, e] = v[1]
    return (c.reshape(128, -1), s)
def pk(c, s):
    return (np.ascontiguousarray(c), mx_ref.live(s))
def emit(q):
    return q[0], q[1]
def packed(v, rng):
    q = [mx_ref.quantize(np.ascontiguousarray(v[r])) for r in range(N)]
    return np.stack([a for a, b in q]), np.stack([mx_ref.plane(b, rng) for a, b in q])
def values_of_codes():
    e, c = np.zeros((128, 128, 4), np.float32), np.zeros((128, 2, 4), np.uint8)
    e[np.arange(128), np.arange(128), 0] = 1
    c[:127, :, 0] = np.arange(256).reshape(2, 128).T[:127]
    return mx_ref.matmul(mx_ref.quantize(e.reshape(128, 512).astype(BF)), (c.reshape(128, 8), np.full((16, 2), 127, np.uint8))).T.reshape(-1).astype(np.float64)
CODE_VALUE, SCALE_VALUE = values_of_codes(), 2.0 ** (np.arange(256) - 127.0)
def decode(q):
    return (CODE_VALUE[q[0]].reshape(16, 8, -1, 4) * SCALE_VALUE[q[1]][:, None, :, None] + 0.0).reshape(128, -1).astype(np.float32)
def f(rng, *shape):
    return mx_ref.flush((rng.standard_normal(shape, dtype=np.float32) * np.exp2(rng.integers(-2, 3, shape[:-1] + (1,)))).astype(BF))
def wide(rng, *shape, cols=0):
    v = rng.standard_normal(shape, dtype=np.float32) * np.exp2(rng.integers(-12, 13, shape)).astype(np.float32)
    if cols: v *= np.repeat(np.exp2(rng.integers(-cols, cols + 1, shape[:-2] + (1, shape[-1] // 4))) * (rng.random(shape[:-2] + (1, shape[-1] // 4)) > 0.0625), 4, axis=-1).astype(np.float32)
    return mx_ref.flush(v.astype(BF))
C, R = 288, 2
M = N * C
def numbers_of(rng):
    return {"x": np.array(f(rng, N, 128, 4 * C)), "u": np.array(f(rng, N, 128, 512)), "v": np.array(f(rng, N, 128, 512))}
def weights(rng, w):
    c, p = packed(w, rng)
    return {"wc": c, "ws": p}
def still(rng):
    w = np.zeros((N, 128, 4, 128, 4), np.float32)
    i = np.arange(128)
    for b in range(4): w[:, i, b, i, b] = 32
    return weights(rng, w.reshape(N, 128, 2048).astype(BF))
def anywhere(rng):
    return rng.integers(0, M, (4, M))
def stored(e):
    return np.stack([table(e[:, C * r:C * r + C].reshape(-1)) for r in range(N)])
def signs(rng):
    return rng.permutation(N) % 2 * 2.0 - 1.0
def setup_inputs(rng):
    return {**numbers_of(rng), **weights(rng, f(rng, N, 128, 2048)), "sc": stored(anywhere(rng))}
def setup_inputs_ties(rng):
    d = numbers_of(rng)
    x = d["x"].reshape(N, 128, C, 4)
    a = x[0, :8, :3].copy()
    a[:, 2] = 0
    for r in range(N): x[r, :8] = a[:, rng.permutation(C) % 3]
    u = d["u"].reshape(N, 128, 128, 4)
    u[:, :8, 0] = u[0, :8, 0].copy()
    u[:, 8:, 0] = 0
    w = np.array(f(rng, 128, 2048)).reshape(128, 4, 128, 4)
    w[8:, :, :8] = 0
    return {"x": x.reshape(N, 128, 4 * C), "u": u.reshape(N, 128, 512), "v": d["v"], **weights(rng, np.stack([w.reshape(128, 2048)] * N)), "sc": stored(anywhere(rng))}
def setup_inputs_near(rng):
    d = numbers_of(rng)
    g = signs(rng)
    low = np.repeat(g < 0, C)
    o = np.concatenate([rng.permutation(np.flatnonzero(low)), rng.permutation(np.flatnonzero(~low))])
    place = np.argsort(o)
    s = place % (M // 2)
    x = np.abs(d["x"].astype(np.float32)).reshape(N, 128, C, 4)
    v = (((s[:, None] >> np.arange(12)) & 1) * np.exp2(np.arange(12) - 23.0)).reshape(N, C, 12)
    x[:, :8] = 0
    x[:, 0, :, 0] = 1
    for i in range(3): x[:, 8 + i] = v[:, :, 4 * i:4 * i + 4]
    x[:, 11:16] = rng.integers(4, 8, (N, 5, C, 4)) * 2.0 ** -20
    u = d["u"].reshape(N, 128, 128, 4)
    u[:, :, 0] = 0
    u[:, 0, 0, 0] = g.astype(np.float32).astype(BF)
    u[:, 8:11, 0] = 1
    c = rng.permutation(M)
    after = np.zeros(M, int)
    after[c] = np.roll(c, -1)
    e = np.stack([o[np.maximum(place[after] - i, 0)] for i in range(4)])
    e = np.take_along_axis(e, np.argsort(rng.random((4, M)), axis=0), axis=0)
    k = np.flatnonzero(place[after] >= M // 2 + 4)[::2]
    a = place[after[k]]
    e[:, k] = o[np.stack([a - M // 2 - 4, a - 1, a, a - 2])]
    return {"x": x.reshape(N, 128, 4 * C).astype(BF), "u": u.reshape(N, 128, 512), "v": d["v"], **still(rng), "sc": stored(e)}
def setup_inputs_huge(rng):
    d = numbers_of(rng)
    g = signs(rng)
    x = 2.0 ** 30 * (0.6 + 0.4 * rng.random((N, 128, 4 * C)))
    u = d["u"].reshape(N, 128, 128, 4)
    a = 2.0 ** 30 * (1 - 0.25 * rng.random((N, 128, 4))) * g[:, None, None]
    u[:, :, 0] = a.astype(np.float32).astype(BF)
    minus, plus = np.flatnonzero(np.repeat(g < 0, C)), np.flatnonzero(np.repeat(g > 0, C))
    e = anywhere(rng)
    k = np.concatenate([rng.permutation(C) % 3 for r in range(N)])
    e[:, k == 0] = minus[e[:, k == 0] % (M // 2)]
    e[:, k == 1] = plus[e[:, k == 1] % (M // 2)]
    return {"x": x.astype(np.float32).astype(BF), "u": u.reshape(N, 128, 512), "v": d["v"], **still(rng), "sc": stored(e)}
def setup_inputs_one(rng):
    d = numbers_of(rng)
    x = d["x"].reshape(N, 128, C, 4)
    u = d["u"].reshape(N, 128, 128, 4)
    w = np.array(f(rng, N, 128, 2048)).reshape(N, 128, 4, 128, 4)
    for i, k in ((0, 2 ** 23), (127, -2 ** 23)):
        x[:, i] = 0
        x[:, i, :, 0] = 4
        u[:, i, 0] = 0
        u[:, i, 0, 0] = k
        w[:, i] = 0
        w[:, i, :, :, 0] = k
    for i in (0, 127):
        w[:, :, :, i] = 0
        w[:, i, 0, i, 0] = 32
    a = C * rng.permutation(N)
    e = a[0] + rng.integers(0, C, (4, M))
    e[:, a[1]:a[1] + C] = a[0] + rng.permutation(C)
    e[:, a[2]:a[2] + C] = e[:, a[2]:a[2] + 1].copy()
    c = a[0] + rng.permutation(C)
    e[:, c[:-1]] = np.roll(c[:-1], -1)
    e[:, c[-1]] = c[-1]
    return {"x": x.reshape(N, 128, 4 * C), "u": u.reshape(N, 128, 512), "v": d["v"], **weights(rng, w.reshape(N, 128, 2048)), "sc": stored(e)}
def setup_inputs_spread(rng):
    d = setup_inputs(rng)
    d["x"] = wide(rng, N, 128, 4 * C, cols=6)
    return d
def check_inputs(d):
    b = []
    for k in ("x", "u", "v"):
        a = np.abs(d[k].astype(np.float32))
        if not (np.isfinite(a).all() and ((a == 0) | (a >= 2.0 ** -30) & (a <= 2.0 ** 30)).all()): b.append("a value of " + k)
    if ((d["sc"] < 0) | (d["sc"] >= M)).any(): b.append("an entry of sc")
    return b
def reference(x, u, v, wc, ws, sc):
    qu = [mx_ref.quantize(u[r]) for r in range(N)]
    lay = [pk(wc[r], ws[r]) for r in range(N)]
    follow = np.concatenate([entries(sc[r]).reshape(4, C) for r in range(N)], axis=1)
    now = [x[r] for r in range(N)]
    for t in range(R):
        q = [mx_ref.quantize(now[r]) for r in range(N)]
        s = np.concatenate([mx_ref.matmul(qu[r], q[r])[0] for r in range(N)]) + np.float32(0.0)
        p = [follow[np.argmax(s[follow], axis=0), np.arange(M)]]
        for g in range(7): p.append(p[g][p[g]])
        p = np.stack(p)
        z = decode(join(*q)).astype(BF)
        z = decode(mx_ref.quantize(z)).astype(BF)
        now = []
        for r in range(N):
            h = mx_ref.quantize(gcols(z, p[:, C * r:C * r + C]))
            now.append(tile([np.maximum(mx_ref.matmul(pick(lay[r], np.arange(128 * b, 128 * b + 128)), h), np.float32(0.0)) * np.float32(0.03125) for b in range(4)]))
    y, pl = np.zeros((N, 128, C), np.float32), np.zeros((N, 8, C), np.float32)
    oc, osc = np.zeros((N, 128, 4 * C), np.uint8), np.zeros((N, 16, C), np.uint8)
    for r in range(N):
        last = mx_ref.quantize(now[r])
        y[r] = mx_ref.matmul(mx_ref.quantize(v[r]), last)
        pl[r] = p[:, C * r:C * r + C]
        oc[r], osc[r] = emit(last)
    return {"y": y, "pl": pl, "oc": oc, "osc": osc}

@@ -1,0 +1,591 @@
+from concourse.bass import DstId, RemoteDMATransfer
+from concourse.mybir import dt, AluOpType, ActivationFunctionType
+
+N, C, ROUNDS = 8, 288, 2
+M = N * C
+HALF = M // 2
+OWN = HALF + 32
+TW = HALF + M + 32
+PAD = 128 - 108
+CUT, CUT2 = 384, 864
+Q4, U8, BF, F32, I32, U16 = "float8_e4m3fn_x4", "uint8", "bfloat16", "float32", "int32", "uint16"
+
+
+def _sb(n, d):
+    return ("sbuf", [128, n], d)
+
+
+SCRATCH = {
+    "ub": _sb(512, BF), "vb": _sb(512, BF), "uq": _sb(128, Q4), "us": _sb(128, U8), "vq": _sb(128, Q4), "vs": _sb(128, U8),
+    "wq": _sb(512, Q4), "wp": _sb(512, U8),
+    "ct": _sb(8 * 516, BF), "mq": _sb(32 * 128, Q4), "ms": _sb(32 * 128, U8), "valm": _sb(128, F32), "vale": _sb(128, F32),
+    "st": _sb(M, F32), "srow": _sb(384, F32), "sg": _sb(4 * C, F32), "sv": _sb(4 * C, F32),
+    "o32": _sb(72, I32), "osc16": _sb(72, U16),
+    "gt": _sb(36, F32), "mx": _sb(36, F32), "df": _sb(36, F32), "tt": _sb(36, F32), "nn": _sb(36, F32),
+    "cc": _sb(18, F32), "ee": _sb(18, F32), "ff": _sb(18, F32), "vv": _sb(18, F32), "eb": _sb(72, BF),
+    "xin": _sb(OWN + 32, BF), "t0": _sb(TW, BF), "t1": _sb(TW, BF), "y0": _sb(OWN, BF), "y1": _sb(OWN, BF),
+    "wv": _sb(8 * 96, F32), "of0": _sb(74, U16), "of1": _sb(74, U16), "plt": _sb(256, F32), "plo": _sb(256, F32),
+    "pi": _sb(4, I32), "pf": _sb(8, F32), "qi": _sb(18, F32), "gp": _sb(18, F32), "k1": _sb(18, F32), "k2": _sb(18, I32),
+    "k3": _sb(18, F32), "k4": _sb(18, F32), "tgt": _sb(18, U16),
+    "gs": _sb(C, BF), "ys": _sb(C, BF), "v1": _sb(18, F32), "o1": _sb(18, U16),
+    "ta": _sb(54, F32), "ti": _sb(54, I32), "tm": _sb(54, F32), "co": _sb(54, F32), "f1": _sb(18, F32), "f2": _sb(18, F32),
+    "f3": _sb(18, F32), "oz": _sb(18, U16), "yo": _sb(C, F32),
+    "dsc": ("dram", [N, 128, 9], I32),
+}
+for _t in range(ROUNDS + 1):
+    SCRATCH.update({"x%d" % _t: _sb(4 * C, BF), "xq%d" % _t: _sb(C, Q4), "xs%d" % _t: _sb(C, U8)})
+for _t in range(ROUNDS):
+    for _n in ("s", "g", "zp", "h"):
+        SCRATCH["%sb%d" % (_n, _t)] = _sb(4 * C, BF)
+    for _n, _w in (("s", C), ("a", C), ("g", C), ("b", 2 * PAD + C), ("h", C), ("ra", 72), ("rb", 72)):
+        SCRATCH["%sq%d" % (_n, _t)] = _sb(_w, Q4)
+        SCRATCH["%ss%d" % (_n, _t)] = _sb(_w, U8)
+    SCRATCH["z%d" % _t] = _sb(4 * M, BF)
+    SCRATCH["dx%d" % _t] = ("dram", [16, N, 4 * C], BF)
+    SCRATCH["dl%d" % _t] = ("dram", [N, 128, 3], F32)
+for _b in range(8):
+    SCRATCH["pb%d" % _b] = ("psum", [128, 512], F32)
+
+_PER_ROUND = (["so", "sa", "sr", "d1_", "d2_", "ha", "pd", "raq", "ras", "rbq", "rbs"]
+              + ["zx%d_" % _b for _b in range(4)] + ["hb%d_" % _r for _r in range(N)])
+SEMAPHORES = (["cv", "cs", "cp", "cg", "sent", "lx", "lu", "lv", "lw", "c0", "ca", "c1", "out"]
+              + ["%s%d" % (n, t) for t in range(ROUNDS) for n in _PER_ROUND])
+
+
+def relays_of(core, topo):
+    same = [c for c in topo.cores_of(core) if c != core and topo.die(c) == topo.die(core)]
+    other = [c for c in topo.cores_of(core) if topo.die(c) != topo.die(core)]
+    return [same[0], other[0], same[1], other[1]]
+
+
+def served(src, k):
+    return [r for r in (2 * k, 2 * k + 1) if r != src]
+
+
+def landing(hop, src, t):
+    c0 = PAD + 36 * (src // 2) + (PAD + 144) * (src % 2) if hop == "b" else 36 * src
+    return hop + "q%d" % t, hop + "s%d" % t, c0, ("ha%d" % t if hop == "a" else "hb%d_%d" % (src, t))
+
+
+def transfer(topo, src, dst, engines, sem, s, d):
+    rid, pid = topo.addr(dst, src)
+    return RemoteDMATransfer(dst_ids=[DstId(rid=rid, pnc=pid)], dma_engine_mask=sum(1 << e for e in engines),
+                             remote_sem=sem, src=s, dst=d)
+
+
+def share(engines, k, n):
+    w = len(engines) // n
+    return engines[w * k:w * k + w]
+
+
+def relay_program(g, core, T, topo, src, k):
+    sent = 0
+    fed = len(share(topo.engines(T.cores[src], core), k, 4))
+    to = served(src, k)
+    for t in range(ROUNDS):
+        for hop in "ab":
+            lq, ls, c0, sem = landing(hop, src, t)
+            for kind in "qs":
+                g.wait_ge(T.sem["r%s%s%d" % (hop, kind, t)], fed)
+                ts = []
+                for i, r in enumerate(to):
+                    o = 36 * (r - 2 * k)
+                    s, d = T["r%s%s%d" % (hop, kind, t)][:, o:o + 36], T[lq if kind == "q" else ls][:, c0:c0 + 36]
+                    if kind == "q":
+                        s, d = s.bitcast(dt.uint8), d.bitcast(dt.uint8)
+                    eng = share(topo.engines(core, T.cores[r]), i, len(to))
+                    ts.append(transfer(topo, core, T.cores[r], eng, T.sem[sem], s, d))
+                    sent += len(eng)
+                g.remote_dma_fused(ts, local_sem=T.sem.sent)
+    g.wait_ge(T.sem.sent, sent)
+
+
+def rank_program(g, core, T, topo):
+    me = T.rank_of(core)
+    if me is None:
+        for r in range(N):
+            if core in relays_of(T.cores[r], topo):
+                relay_program(g, core, T, topo, r, relays_of(T.cores[r], topo).index(core))
+        return
+    A, ACT = AluOpType, ActivationFunctionType
+    queue = {"v": g.vector, "s": g.scalar, "p": g.tensor, "g": g, "y": g.sync}
+    done = {e: {"sem": "c" + e, "n": 0} for e in "vspg"}
+    waited = {e: {} for e in queue}
+    log = {}
+    groups = {}
+
+    def R(name, c0=0, c1=None, step=1, p0=0, p1=128):
+        if c1 is None:
+            c1 = SCRATCH[name][1][-1]
+        return (name, p0, p1, c0, c1, step)
+
+    def ap(r):
+        return T[r[0]][r[1]:r[2], r[3]:r[4]:r[5]] if r[5] > 1 else T[r[0]][r[1]:r[2], r[3]:r[4]]
+
+    def meet(a, b):
+        if a[2] <= b[1] or b[2] <= a[1] or a[4] <= b[3] or b[4] <= a[3]:
+            return False
+        if a[5] == b[5]:
+            return (a[3] - b[3]) % a[5] == 0
+        return bool(set(range(a[3], a[4], a[5])) & set(range(b[3], b[4], b[5])))
+
+    def wait(e, tok):
+        if tok[1] is None:
+            grp = groups[tok[0]]
+            grp["shut"] = True
+            n = grp["n"]
+        else:
+            n = tok[1]
+        if waited[e].get(tok[0], 0) < n:
+            queue[e].wait_ge(T.sem[tok[0]], n)
+            waited[e][tok[0]] = n
+
+    def order(e, reads, writes, own=None, adds=False):
+        need = {}
+        for r, w in [(r, False) for r in reads] + [(r, True) for r in writes]:
+            bank = r[0].startswith("pb")
+            if bank and adds:
+                continue
+            for (o, ow, tok, oe) in log.get(r[0], []):
+                if tok[0] == own:
+                    continue
+                if (bank and (oe != e or w or ow)) or (not bank and (w or ow) and meet(r, o)):
+                    if tok[1] is None or need.get(tok[0], 0) < tok[1]:
+                        need[tok[0]] = tok[1]
+        for s in need:
+            wait(e, (s, need[s]))
+
+    def note(e, tok, reads, writes):
+        for r in reads:
+            log.setdefault(r[0], []).append((r, False, tok, e))
+        for r in writes:
+            log.setdefault(r[0], []).append((r, True, tok, e))
+
+    def op(e, call, reads, writes, adds=False):
+        order(e, reads, writes, adds=adds)
+        done[e]["n"] += 1
+        call().then_inc(T.sem[done[e]["sem"]], 1)
+        note(e, (done[e]["sem"], done[e]["n"]), reads, writes)
+
+    def more(name, n):
+        grp = groups.setdefault(name, {"n": 0, "shut": False})
+        assert not grp["shut"], name
+        grp["n"] += n
+
+    def dma(e, name, out, in_, reads, writes):
+        order(e, reads, writes, own=name)
+        more(name, 16)
+        queue[e].dma_start(out, in_).then_inc(T.sem[name], 16)
+        note(e, (name, None), reads, writes)
+
+    def bits(r):
+        return ap(r).bitcast(dt.uint8)
+
+    others = [r for r in range(N) if r != me]
+    relays = relays_of(core, topo)
+
+    def remote(ts, n, reads):
+        order("g", reads, [])
+        g.remote_dma_fused(ts, local_sem=T.sem.sent)
+        more("sent", n)
+        note("g", ("sent", None), reads, [])
+
+    def spread(piece, reads, sem):
+        remote([transfer(topo, core, T.cores[r], [topo.engines(core, T.cores[r])[i]], T.sem[sem], piece, piece)
+                for i, r in enumerate(others)], len(others), reads)
+
+    def arrives(sem, n, writes):
+        more(sem, n)
+        note("g", (sem, None), [], writes)
+
+    def val(x):
+        return ap(x) if isinstance(x, tuple) else x
+
+    def copy(e, out, in_, offs=None):
+        src = ap(in_) if offs is None else ap(in_).indirect(ap(offs))
+        rd = [in_] if offs is None else [in_, offs]
+        if e == "v":
+            op(e, lambda: g.vector.tensor_copy(ap(out), src), rd, [out])
+        elif e == "g":
+            wait(e, ("cg", done[e]["n"]))
+            op(e, lambda: g.affine_select(ap(out), src, [[0, in_[4] - in_[3]]], A.is_gt, 0.0, 1, 0), rd, [out])
+        else:
+            op(e, lambda: g.scalar.activation(ap(out), src, ACT.Copy), rd, [out])
+
+    def tt(out, a, b, alu):
+        op("v", lambda: g.vector.tensor_tensor(ap(out), ap(a), ap(b), alu), [a, b], [out])
+
+    def ts(out, a, s1, o1, s2=None, o2=None):
+        rd = [a] + [s for s in (s1, s2) if isinstance(s, tuple)]
+        if s2 is None:
+            op("v", lambda: g.vector.tensor_scalar(ap(out), ap(a), val(s1), None, o1), rd, [out])
+        else:
+            op("v", lambda: g.vector.tensor_scalar(ap(out), ap(a), val(s1), val(s2), o1, o2), rd, [out])
+
+    def fill(out, c):
+        op("v", lambda: g.vector.memset(ap(out), c), [], [out])
+
+    def turn(out, in_):
+        op("v", lambda: g.vector.transpose(ap(out), ap(in_)), [in_], [out])
+
+    def quant(q, s, in_):
+        op("v", lambda: g.vector.quantize_mx(ap(q), ap(s), ap(in_)), [in_], [q, s])
+
+    def mm(bank, wq, ws, xq, xs, start=True, stop=True):
+        out = R("pb%d" % bank, 0, xq[4] - xq[3])
+        op("p", lambda: g.tensor.matmul_mx(ap(out), ap(wq), ap(ws), ap(xq), ap(xs), start, stop), [wq, ws, xq, xs], [out],
+           adds=not start)
+
+    def const(k):
+        return R("mq", 128 * k, 128 * k + 128), R("ms", 128 * k, 128 * k + 128)
+
+    def iota(out, pattern, base, cm):
+        if SCRATCH[out[0]][2] != I32:
+            op("g", lambda: g.iota(ap(out), pattern, base, cm, allow_small_or_imprecise_dtypes=True), [], [out])
+        else:
+            op("g", lambda: g.iota(ap(out), pattern, base, cm), [], [out])
+
+    def plus(out, in_, c):
+        op("s", lambda: g.scalar.activation(ap(out), ap(in_), ACT.Identity, bias=c), [in_], [out])
+
+    def slot(name, k):
+        return (name, 0, 128, k, k + 1, 1)
+
+    def slots(name):
+        return (name, 0, 128, 0, N, 1)
+
+    SH0, SH1, SHZ = R("pf", 4, 5), R("pf", 5, 6), R("pf", 6, 7)
+
+    def parts_out(t):
+        for k in range(N):
+            src = T.x[16 * k:16 * k + 16, :] if t == 0 else T["x%d" % t][16 * k:16 * k + 16, :]
+            dma("y", "d1_%d" % t, T["dx%d" % t][:, k, :], src,
+                [] if t == 0 else [R("x%d" % t, p0=16 * k, p1=16 * k + 16)], [slot("dx%d" % t, k)])
+
+    def parts_in(t):
+        wait("y", ("so%d" % t, None))
+        for d in range(N):
+            dma("y", "d2_%d" % t, T["sb%d" % t][16 * d:16 * d + 16, :], T["dx%d" % t][:, :, 144 * d:144 * d + 144],
+                [slots("dx%d" % t)], [R("sb%d" % t, p0=16 * d, p1=16 * d + 16)])
+
+    def hop(src, name, t):
+        sq, ss = src + "q%d" % t, src + "s%d" % t
+        for kind, buf, view in (("q", sq, bits), ("s", ss, ap)):
+            to = "r%s%s%d" % (name, kind, t)
+            engs = [share(topo.engines(core, c), k, 4) for k, c in enumerate(relays)]
+            remote([transfer(topo, core, c, engs[k], T.sem[to], view(R(buf, 72 * k, 72 * k + 72)), view(R(to)))
+                    for k, c in enumerate(relays)], sum(len(e) for e in engs), [R(buf)])
+        lq, ls, c0, sem = landing(name, me, t)
+        a, b = R(sq, 36 * me, 36 * me + 36), R(ss, 36 * me, 36 * me + 36)
+        dma("y", sem, bits(R(lq, c0, c0 + 36)), bits(a), [a], [R(lq, c0, c0 + 36)])
+        dma("y", sem, ap(R(ls, c0, c0 + 36)), ap(b), [b], [R(ls, c0, c0 + 36)])
+        for r in others:
+            lq, ls, c0, sem = landing(name, r, t)
+            via = relays_of(T.cores[r], topo)[me // 2]
+            arrives(sem, 2 * len(share(topo.engines(via, core), 0, len(served(r, me // 2)))),
+                    [R(lq, c0, c0 + 36), R(ls, c0, c0 + 36)])
+
+    def score(t):
+        xq, xs = R("xq%d" % t), R("xs%d" % t)
+        quant(xq, xs, R("x%d" % t))
+        if t == 0:
+            quant(R("uq"), R("us"), R("ub"))
+        mm(7, R("uq"), R("us"), xq, xs)
+        copy("s", R("srow", 0, C, p1=1), R("pb7", 0, C, p1=1))
+        dl = "dl%d" % t
+        dma("s", "so%d" % t, T[dl][me], T.srow[0:1, :], [R("srow", p1=1)], [slot(dl, me)])
+        spread(T[dl][me], [slot(dl, me)], "sa%d" % t)
+        arrives("sa%d" % t, N - 1, [slot(dl, r) for r in others])
+
+    def score_rows(t):
+        for k in range(8):
+            dma("ys"[k % 2], "sr%d" % t, T.st[16 * k:16 * k + 1, :], T["dl%d" % t][:, 0:96, :],
+                [slots("dl%d" % t)], [R("st", p0=16 * k, p1=16 * k + 1)])
+
+    def hop1(t):
+        quant(R("sq%d" % t), R("ss%d" % t), R("sb%d" % t))
+        wait("g", ("sr%d" % t, None))
+        hop("s", "a", t)
+
+    def pad(t):
+        a, b = R("xq0", 0, PAD), R("xs0", 0, PAD)
+        for c in (0, PAD + 144):
+            dma("y", "pd%d" % t, bits(R("bq%d" % t, c, c + PAD)), bits(a), [a], [R("bq%d" % t, c, c + PAD)])
+            dma("y", "pd%d" % t, ap(R("bs%d" % t, c, c + PAD)), ap(b), [b], [R("bs%d" % t, c, c + PAD)])
+
+    def movers(first, src, wanted):
+        fill(R("ct", 516 * first, 516 * first + 4 * 516), 0.0)
+        for i, w in enumerate(wanted):
+            d = first + i
+            ts(R("ct", 516 * d + 3, 516 * d + 515, 4), R(src), float(w), A.is_equal)
+        for k in range(4 * first, 4 * first + 16):
+            o = 516 * (k // 4) + 3 - k % 4
+            quant(*const(k), R("ct", o, o + 512))
+
+    def columns():
+        for p0, lo in ((0, True), (64, False)):
+            fill(R("pf", 4, 5, p0=p0, p1=p0 + 64), float(HALF) if lo else 0.0)
+            fill(R("pf", 6, 7, p0=p0, p1=p0 + 64), -32.0 if lo else HALF - 32.0)
+            fill(R("co", 0, 18, p0=p0, p1=p0 + 64), -9 * 252.0 if lo else 2 * M - 9 * 252.0)
+            fill(R("co", 36, 54, p0=p0, p1=p0 + 64), 0.0 if lo else -float(M))
+        fill(R("co", 18, 36), 252.0)
+        sh = 4 if me else 5
+        ts(R("pi", 1, 2), R("pi", 0, 1), (1 << sh) - 1, A.bitwise_and)
+        ts(R("pi", 2, 3), R("pi", 0, 1), sh, A.arith_shift_right)
+        ts(R("pi", 3, 4), R("pi", 0, 1), 16, A.bitwise_and)
+        copy("v", R("pf", 0, 4), R("pi"))
+        tt(SH1, SH0, R("pf", 3, 4), A.subtract)
+        ts(R("pf", 7, 8), R("pf", 2, 3), 36.0 if me else 72.0, A.mult, SH0 if me < 2 else SH1, A.add)
+        ts(R("qi"), R("qi"), R("pf", 1, 2), A.add)
+        ts(R("k1"), R("qi"), -17.5, A.add, 1.0 / 36, A.mult)
+        tt(R("k4"), R("qi"), R("gp"), A.add)
+        copy("v", R("k2"), R("k1"))
+        ts(R("k3"), R("k2"), 252.0, A.mult, R("pf", 7, 8), A.add)
+        tt(R("k1"), R("k3"), R("k4"), A.add)
+        copy("v", R("tgt"), R("k1"))
+
+    def first_list():
+        cuts = (0, 320, 608, 896, 4 * C)
+        for i, e in enumerate("vsss"):
+            copy(e, R("sg", cuts[i], cuts[i + 1]), R("st"), R("osc16", cuts[i] // 16, cuts[i + 1] // 16))
+        for i in range(4):
+            turn(R("sv", cuts[i], cuts[i + 1]), R("sg", cuts[i], cuts[i + 1]))
+        sa, sb = R("sv", 0, 576, 16), R("sv", 576, 1152, 16)
+        na, nb = R("sv", 1, 576, 16), R("sv", 577, 1152, 16)
+        tt(R("gt"), sb, sa, A.is_gt)
+        tt(R("df"), nb, na, A.subtract)
+        tt(R("mx"), sb, sa, A.max)
+        tt(R("tt"), R("gt"), R("df"), A.mult)
+        tt(R("cc"), R("mx", 18, 36), R("mx", 0, 18), A.is_gt)
+        tt(R("nn"), R("tt"), na, A.add)
+        tt(R("ee"), R("nn", 18, 36), R("nn", 0, 18), A.subtract)
+        tt(R("ff"), R("ee"), R("cc"), A.mult)
+        for e in (0, 1):
+            tt(R("vv", 9 * e, 9 * e + 9), R("ff", e, 18, 2), R("nn", e, 18, 2), A.add)
+        copy("v", R("eb", 0, 72, 4), R("vv"))
+        copy("v", R("eb", 2, 72, 4), R("vv"))
+        tt(R("eb", 1, 72, 4), R("vv"), R("eb", 0, 72, 4), A.subtract)
+        tt(R("eb", 3, 72, 4), R("vv"), R("eb", 0, 72, 4), A.subtract)
+        k = 0
+        for q in range(4):
+            for a, c0, c1, b0 in ([(0, 0, 18, 1), (1, 0, 18, 19), (2, 0, 1, 37)] if q < 2 else
+                                  [(2, 0, 18, 1), (3, 0, 18, 19), (1, 17, 18, 0)]):
+                copy("vs"[k % 2], R("xin", 32 * b0, 32 * (b0 + c1 - c0), 8, 32 * q, 32 * q + 32),
+                     R("eb", 4 * c0, 4 * c1, 1, 32 * a, 32 * a + 32))
+                k += 1
+        turn(R("t0", HALF, HALF + OWN + 32), R("xin"))
+
+    def double(l):
+        new, old, off = "t%d" % (l % 2), "t%d" % (1 - l % 2), "of%d" % (1 - l % 2)
+        for e, a, b in (("v", 0, CUT), ("s", CUT, CUT2), ("s", CUT2, OWN)):
+            copy(e, R(new, HALF + a, HALF + b), R(old), R(off, a // 16, b // 16))
+
+    def swap_lo(l, e, a, b):
+        t = "t%d" % (l % 2)
+        copy(e, R(t, a, b, p0=64), R(t, HALF + a, HALF + b, p1=64))
+
+    def swap_hi(l, e, a, b):
+        t = "t%d" % (l % 2)
+        copy(e, R(t, HALF + OWN + a, HALF + OWN + b, p1=64), R(t, OWN + a, OWN + b, p0=64))
+
+    def wrap(l, swap=False):
+        t, w = "t%d" % (l % 2), 96 * l
+        if l == 0:
+            turn(R("y0"), R(t, HALF, HALF + OWN))
+            turn(R("y1"), R(t, HALF + 16, HALF + OWN + 16))
+            tt(R("wv", 0, 74, 2), R("y0", 0, OWN, 32), R("y0", 8, OWN, 32), A.add)
+            tt(R("wv", 1, 74, 2), R("y1", 0, OWN, 32), R("y1", 8, OWN, 32), A.add)
+        else:
+            for a, b in ((0, CUT), (CUT, CUT2), (CUT2, OWN)):
+                turn(R("y0", a, b), R(t, HALF + a, HALF + b))
+                if swap and b < OWN:
+                    swap_hi(l, "v", max(a - 32, 0), b - 32)
+            tt(R("wv", w, w + 74), R("y0", 0, OWN, 16), R("y0", 8, OWN, 16), A.add)
+        if l < 7:
+            ts(R("of%d" % (l % 2)), R("wv", w, w + 74), SH1 if l else SH0, A.add)
+        if swap:
+            swap_hi(l, "v", CUT2 - 32, HALF)
+
+    def unpack(t, todo, n, engines):
+        for i in range(min(n, len(todo))):
+            j = todo.pop(0)
+            b, d = j // 4, j % 4
+            z = "z%d" % t
+            mm(j % 7, *const(4 * d + b), R("aq%d" % t), R("as%d" % t))
+            copy(engines[i % len(engines)], R(z, M * b + C * d, M * b + C * d + C), R("pb%d" % (j % 7), 0, C))
+            if d == 3:
+                for p in (0, 64):
+                    o, s = R(z, M * b + HALF, M * b + M, 1, p, p + 64), R(z, M * b, M * b + HALF, 1, 64 - p, 128 - p)
+                    dma("y", "zx%d_%d" % (b, t), ap(o), ap(s), [s], [o])
+
+    def look(table, off):
+        copy("v", R("gs", 0, 128), R(table), R(off, 0, 8))
+        copy("s", R("gs", 128, C), R(table), R(off, 8, 18))
+        turn(R("ys"), R("gs"))
+        tt(R("v1"), R("ys", 0, C, 16), R("ys", 8, C, 16), A.add)
+
+    def places(l):
+        table = "t%d" % (l % 2)
+        look(table, "tgt")
+        if me:
+            ts(R("o1"), R("v1"), SH1 if l else SH0, A.add)
+            look(table, "o1")
+        for k, w in enumerate((C, 36, 144)):
+            ts(R("ta", 18 * k, 18 * k + 18), R("v1"), -(32 + (w - 1) / 2.0), A.add, 1.0 / w, A.mult)
+        copy("v", R("ti"), R("ta"))
+        tt(R("tm"), R("ti"), R("co"), A.mult)
+        tt(R("f1"), R("tm", 0, 18), R("tm", 18, 36), A.add)
+        tt(R("f2"), R("tm", 36, 54), R("v1"), A.add)
+        tt(R("f3"), R("f1"), R("f2"), A.add)
+        ts(R("oz"), R("f3"), SHZ, A.add)
+
+    def serve(t):
+        for b in range(4):
+            copy("sv"[b % 2], R("gb%d" % t, b, 4 * C, 4), R("z%d" % t, M * b, M * b + M), R("oz"))
+        quant(R("gq%d" % t), R("gs%d" % t), R("gb%d" % t))
+        hop("g", "b", t)
+
+    def take(t, k0, k1):
+        zp, h = "zpb%d" % t, "hb%d" % t
+        for f in (0, 1):
+            c1 = PAD + (PAD + 144) * f + 36 * k1
+            for i in range(8):
+                mm(i, *const(16 + 4 * (2 * (i // 4) + f) + i % 4), R("bq%d" % t, c1 - 128, c1), R("bs%d" % t, c1 - 128, c1),
+                   f == 0, f == 1)
+        for i in range(8):
+            e, b = i // 4, i % 4
+            for k in range(k0, k1):
+                o = 128 - 36 * (k1 - k)
+                copy("vs"[i % 2], R(zp, C * k + 144 * e + b, C * k + 144 * e + 144, 4), R("pb%d" % i, o, o + 36))
+        for k in range(k0, k1):
+            for a in range(4):
+                copy("vsvv"[a], R(h, C * a, C * a + C, 1, 32 * k, 32 * k + 32), R(zp, C * k, C * k + C, 1, 32 * a, 32 * a + 32))
+
+    def layer(t):
+        quant(R("hq%d" % t), R("hs%d" % t), R("hb%d" % t))
+        for b in range(4):
+            mm(b, R("wq", 128 * b, 128 * b + 128), R("wp", 128 * b, 128 * b + 128), R("hq%d" % t), R("hs%d" % t))
+        for b in range(4):
+            out, src = R("x%d" % (t + 1), b, 4 * C, 4), R("pb%d" % b, 0, C)
+            if b % 2:
+                op("s", lambda: g.scalar.activation(ap(out), ap(src), ACT.Relu, scale=0.03125), [src], [out])
+            else:
+                ts(out, src, 0.0, A.max, 0.03125, A.mult)
+
+    def lists_out():
+        c0, p0 = 18 * (me % 4) + 2, 64 * (me // 4)
+        for l in range(8):
+            turn(R("plt", 32 * l, 32 * l + 32), R("wv", 96 * l + c0, 96 * l + c0 + 32))
+        ts(R("plo"), R("plt"), -32.0, A.add)
+        for l in range(8):
+            s = R("plo", 32 * l, 32 * l + 16, 1, p0, p0 + 18)
+            dma("y", "out", T.pl[l:l + 1, :], ap(s), [s], [])
+
+    dma("y", "lx", T.x0[:], T.x[:], [], [R("x0")])
+    dma("s", "c0", T.dsc[me], T.sc[:], [], [slot("dsc", me)])
+    dma("y", "lu", T.ub[:], T.u[:], [], [R("ub")])
+    iota(R("st", 0, 576), [[1, 576]], 32, 0)
+    iota(R("valm"), [[-64, 2], [0, 4], [-1, 16]], 0, 1)
+    iota(R("pi", 0, 1), [[0, 1]], 0, 1)
+    spread(T.dsc[me], [slot("dsc", me)], "ca")
+    arrives("ca", N - 1, [slot("dsc", r) for r in others])
+    if me:
+        iota(R("qi"), [[16, 18]], 0, 0)
+        iota(R("gp"), [[0, 18]], 32, 0)
+    else:
+        iota(R("qi"), [[32, 9], [0, 2]], 0, 0)
+        iota(R("gp"), [[0, 9], [36, 2]], 32, 0)
+    iota(R("vale"), [[-32, 4], [256, 2], [-1, 16]], 0, 1)
+    fill(R("srow", C, 384, p1=32), 0.0)
+    fill(R("xin"), 16.0)
+    plus(R("st", 576, HALF), R("st", 0, 576), 576.0)
+    plus(R("st", HALF, M), R("st", 0, HALF), float(HALF))
+
+    for t in range(ROUNDS):
+        last = t == ROUNDS - 1
+        parts_out(t)
+        score(t)
+        if t == 0:
+            for k in (0, 1):
+                copy("s", R("t%d" % k, 0, HALF, p1=64), R("xin", 0, HALF, p1=64))
+                copy("s", R("t%d" % k, HALF + OWN, TW, p0=64), R("xin", 0, HALF, p0=64))
+            dma("y", "c1", T.o32[:], T.dsc[:], [slots("dsc")], [R("o32")])
+            columns()
+            movers(0, "valm", [0, 16, 32, 48])
+            for k, kk in enumerate((0, 2, 1, 3)):
+                copy("v", R("osc16", 18 * k, 18 * k + 18), R("o32", 18 * kk, 18 * kk + 18))
+        parts_in(t)
+        score_rows(t)
+        hop1(t)
+        if t == 0:
+            wait("y", ("ha0", None))
+            dma("y", "lw", bits(R("wq")), T.wc[:], [], [R("wq")])
+            dma("y", "lw", T.wp[:], T.ws[:], [], [R("wp")])
+            dma("y", "lv", T.vb[:], T.v[:], [], [R("vb")])
+            pad(0)
+            pad(1)
+        first_list()
+        todo = list(range(16))
+        mine = max(me - 1, 0)
+        send = max(mine, 3) if last else mine
+        early = 1 if send < 5 else 2
+        for l in range(8 if last else mine + 1):
+            if l:
+                double(l)
+            if l < 7:
+                swap_lo(l, "g", 0, 256 if l == mine else CUT)
+            if l == mine:
+                swap_hi(l, "v", 0, CUT - 32)
+                swap_lo(l, "s", CUT2, HALF)
+                swap_hi(l, "v", CUT - 32, CUT2 - 32)
+                swap_lo(l, "v", 256, CUT2)
+                swap_hi(l, "v", CUT2 - 32, HALF)
+                if l == send:
+                    unpack(t, todo, 16, "sv")
+                places(l)
+                if l == send:
+                    serve(t)
+                elif l >= early:
+                    unpack(t, todo, 8, "s")
+                if last:
+                    wrap(l)
+                continue
+            if l == 7:
+                wrap(l)
+            elif l == 0:
+                swap_lo(l, "s", CUT, HALF)
+                swap_hi(l, "s", 576, HALF)
+                wrap(l)
+                swap_hi(l, "v", 0, 576)
+            elif todo and l >= early:
+                unpack(t, todo, {6: 4, 5: 6, 4: 6}.get(send, 8), "s")
+                swap_lo(l, "g", CUT, 704)
+                wrap(l, True)
+                swap_lo(l, "v", 704, HALF)
+            else:
+                swap_lo(l, "s", CUT, HALF)
+                wrap(l, True)
+            if l == send:
+                serve(t)
+        if t == 0:
+            movers(4, "vale", [0, 256, 16, 272])
+            fill(R("wv"), 0.0)
+            quant(R("vq"), R("vs"), R("vb"))
+        if last:
+            lists_out()
+        take(t, 0, 3)
+        take(t, 3, 4)
+        layer(t)
+
+    xq, xs = R("xq%d" % ROUNDS), R("xs%d" % ROUNDS)
+    quant(xq, xs, R("x%d" % ROUNDS))
+    mm(7, R("vq"), R("vs"), xq, xs)
+    dma("y", "out", T.oc[:], bits(xq), [xq], [])
+    copy("s", R("yo"), R("pb7", 0, C))
+    dma("s", "out", T.y[:], T.yo[:], [R("yo")], [])
+    for k in range(4):
+        dma("y", "out", T.osc[4 * k:4 * k + 4, :], T[xs[0]][32 * k:32 * k + 4, :], [xs], [])
+    for name in groups:
+        wait("g", (name, None))
+    for e in done:
+        wait("g", (done[e]["sem"], done[e]["n"]))

@@ -4,10 +4,8 @@ from concourse.mybir import dt, AluOpType, ActivationFunctionType
 N, C, ROUNDS = 8, 288, 2
 M = N * C
 HALF = M // 2
-OWN = HALF + 32
-TW = HALF + M + 32
 PAD = 128 - 108
-CUT, CUT2 = 384, 864
+TRADE = C - 16
 Q4, U8, BF, F32, I32, U16 = "float8_e4m3fn_x4", "uint8", "bfloat16", "float32", "int32", "uint16"
 
 
@@ -19,15 +17,16 @@ SCRATCH = {
     "ub": _sb(512, BF), "vb": _sb(512, BF), "uq": _sb(128, Q4), "us": _sb(128, U8), "vq": _sb(128, Q4), "vs": _sb(128, U8),
     "wq": _sb(512, Q4), "wp": _sb(512, U8),
     "ct": _sb(8 * 516, BF), "mq": _sb(32 * 128, Q4), "ms": _sb(32 * 128, U8), "valm": _sb(128, F32), "vale": _sb(128, F32),
-    "st": _sb(M, F32), "srow": _sb(384, F32), "sg": _sb(4 * C, F32), "sv": _sb(4 * C, F32),
+    "st": _sb(M, F32), "tb": _sb(M, F32), "srow": _sb(384, F32), "sg": _sb(4 * C, F32), "sv": _sb(4 * C, F32),
     "o32": _sb(72, I32), "osc16": _sb(72, U16),
     "gt": _sb(36, F32), "mx": _sb(36, F32), "df": _sb(36, F32), "tt": _sb(36, F32), "nn": _sb(36, F32),
-    "cc": _sb(18, F32), "ee": _sb(18, F32), "ff": _sb(18, F32), "vv": _sb(18, F32), "eb": _sb(72, BF),
-    "xin": _sb(OWN + 32, BF), "t0": _sb(TW, BF), "t1": _sb(TW, BF), "y0": _sb(OWN, BF), "y1": _sb(OWN, BF),
-    "wv": _sb(8 * 96, F32), "of0": _sb(74, U16), "of1": _sb(74, U16), "plt": _sb(256, F32), "plo": _sb(256, F32),
+    "cc": _sb(18, F32), "ee": _sb(18, F32), "ff": _sb(18, F32), "vv": _sb(18, F32),
+    "oo": _sb(8 * C, F32), "y0": _sb(C, F32), "of": _sb(18, U16), "pw": _sb(4 * C, F32), "opw": _sb(18, U16),
+    "plt": _sb(C, F32), "pli": _sb(C, I32), "plo": _sb(C, F32),
+    "ci": _sb(18, I32), "cw": _sb(18, F32), "cx": _sb(18, F32), "cy": _sb(18, F32),
     "pi": _sb(4, I32), "pf": _sb(8, F32), "qi": _sb(18, F32), "gp": _sb(18, F32), "k1": _sb(18, F32), "k2": _sb(18, I32),
-    "k3": _sb(18, F32), "k4": _sb(18, F32), "tgt": _sb(18, U16),
-    "gs": _sb(C, BF), "ys": _sb(C, BF), "v1": _sb(18, F32), "o1": _sb(18, U16),
+    "k3": _sb(18, F32), "k4": _sb(18, F32), "tgt": _sb(18, U16), "qw": _sb(18, F32),
+    "gs": _sb(C, F32), "ys": _sb(C, F32), "v1": _sb(18, F32), "o1": _sb(18, U16),
     "ta": _sb(54, F32), "ti": _sb(54, I32), "tm": _sb(54, F32), "co": _sb(54, F32), "f1": _sb(18, F32), "f2": _sb(18, F32),
     "f3": _sb(18, F32), "oz": _sb(18, U16), "yo": _sb(C, F32),
     "dsc": ("dram", [N, 128, 9], I32),
@@ -47,8 +46,8 @@ for _b in range(8):
     SCRATCH["pb%d" % _b] = ("psum", [128, 512], F32)
 
 _PER_ROUND = (["so", "sa", "sr", "d1_", "d2_", "ha", "pd", "raq", "ras", "rbq", "rbs"]
-              + ["zx%d_" % _b for _b in range(4)] + ["hb%d_" % _r for _r in range(N)])
-SEMAPHORES = (["cv", "cs", "cp", "cg", "sent", "lx", "lu", "lv", "lw", "c0", "ca", "c1", "out"]
+              + ["zx%d_" % _b for _b in range(4)] + ["hb%d_" % _r for _r in range(N)] + ["bc%d_" % _l for _l in range(7)])
+SEMAPHORES = (["cv", "cs", "cp", "cg", "sent", "lx", "lu", "lv", "lw", "c0", "ca", "c1", "out", "pr"]
               + ["%s%d" % (n, t) for t in range(ROUNDS) for n in _PER_ROUND])
 
 
@@ -206,9 +205,6 @@ def rank_program(g, core, T, topo):
         rd = [in_] if offs is None else [in_, offs]
         if e == "v":
             op(e, lambda: g.vector.tensor_copy(ap(out), src), rd, [out])
-        elif e == "g":
-            wait(e, ("cg", done[e]["n"]))
-            op(e, lambda: g.affine_select(ap(out), src, [[0, in_[4] - in_[3]]], A.is_gt, 0.0, 1, 0), rd, [out])
         else:
             op(e, lambda: g.scalar.activation(ap(out), src, ACT.Copy), rd, [out])
 
@@ -254,7 +250,8 @@ def rank_program(g, core, T, topo):
     def slots(name):
         return (name, 0, 128, 0, N, 1)
 
-    SH0, SH1, SHZ = R("pf", 4, 5), R("pf", 5, 6), R("pf", 6, 7)
+    SHZ = R("pf", 6, 7)
+    turned = me == 1
 
     def parts_out(t):
         for k in range(N):
@@ -310,8 +307,8 @@ def rank_program(g, core, T, topo):
     def pad(t):
         a, b = R("xq0", 0, PAD), R("xs0", 0, PAD)
         for c in (0, PAD + 144):
-            dma("y", "pd%d" % t, bits(R("bq%d" % t, c, c + PAD)), bits(a), [a], [R("bq%d" % t, c, c + PAD)])
-            dma("y", "pd%d" % t, ap(R("bs%d" % t, c, c + PAD)), ap(b), [b], [R("bs%d" % t, c, c + PAD)])
+            dma("g", "pd%d" % t, bits(R("bq%d" % t, c, c + PAD)), bits(a), [a], [R("bq%d" % t, c, c + PAD)])
+            dma("g", "pd%d" % t, ap(R("bs%d" % t, c, c + PAD)), ap(b), [b], [R("bs%d" % t, c, c + PAD)])
 
     def movers(first, src, wanted):
         fill(R("ct", 516 * first, 516 * first + 4 * 516), 0.0)
@@ -322,27 +319,65 @@ def rank_program(g, core, T, topo):
             o = 516 * (k // 4) + 3 - k % 4
             quant(*const(k), R("ct", o, o + 512))
 
+    def table(l):
+        return ("st", 2) if l % 2 else ("tb", 1)
+
+    def rows(l):
+        c0 = C * (l // 2 + 4 * (l % 2))
+        return c0, (table(l - 1)[1] if l else 1)
+
+    def gather(out, c0, src, off):
+        copy("v", R(out, c0, c0 + 128), R(src), R(off, 0, 8))
+        copy("s", R(out, c0 + 128, c0 + C), R(src), R(off, 8, 18))
+
+    def offsets(out, labels, traded):
+        if not traded:
+            ts(R(out), labels, 0.125, A.mult)
+            return
+        ts(R("ci"), labels, 0.125, A.mult)
+        ts(R("cw"), labels, float(TRADE), A.mult, -float(TRADE), A.add)
+        ts(R("cx"), R("ci"), 1.0 - 8 * TRADE, A.mult)
+        tt(R("cy"), R("cw"), R("cx"), A.add)
+        copy("v", R(out), R("cy"))
+
+    def lay(t, l):
+        c0, row = rows(l)
+        name, to = table(l)
+        for d in range(8):
+            dma("ys"[d % 2], "bc%d_%d" % (l, t), T[name][16 * d + to:16 * d + to + 1, :], T.oo[row:128:16, c0:c0 + C],
+                [R("oo", c0, c0 + C)], [R(name, p0=16 * d + to, p1=16 * d + to + 1)])
+
+    def wrap(l):
+        c0, row = rows(l)
+        turn(R("y0"), R("oo", c0, c0 + C))
+        offsets("of", R("y0", row, C, 16), l % 2 == 0)
+
+    def look(src, row, off):
+        gather("gs", 0, src, off)
+        turn(R("ys"), R("gs"))
+        return R("ys", row, C, 16)
+
     def columns():
         for p0, lo in ((0, True), (64, False)):
-            fill(R("pf", 4, 5, p0=p0, p1=p0 + 64), float(HALF) if lo else 0.0)
-            fill(R("pf", 6, 7, p0=p0, p1=p0 + 64), -32.0 if lo else HALF - 32.0)
+            fill(R("pf", 6, 7, p0=p0, p1=p0 + 64), 0.0 if lo else float(HALF))
             fill(R("co", 0, 18, p0=p0, p1=p0 + 64), -9 * 252.0 if lo else 2 * M - 9 * 252.0)
             fill(R("co", 36, 54, p0=p0, p1=p0 + 64), 0.0 if lo else -float(M))
         fill(R("co", 18, 36), 252.0)
-        sh = 4 if me else 5
+        sh = 5 if turned else 4
         ts(R("pi", 1, 2), R("pi", 0, 1), (1 << sh) - 1, A.bitwise_and)
         ts(R("pi", 2, 3), R("pi", 0, 1), sh, A.arith_shift_right)
-        ts(R("pi", 3, 4), R("pi", 0, 1), 16, A.bitwise_and)
+        ts(R("pi", 3, 4), R("pi", 0, 1), 15, A.bitwise_and)
         copy("v", R("pf", 0, 4), R("pi"))
-        tt(SH1, SH0, R("pf", 3, 4), A.subtract)
-        ts(R("pf", 7, 8), R("pf", 2, 3), 36.0 if me else 72.0, A.mult, SH0 if me < 2 else SH1, A.add)
+        ts(R("pf", 7, 8), R("pf", 2, 3), 72.0 if turned else 36.0, A.mult)
         ts(R("qi"), R("qi"), R("pf", 1, 2), A.add)
+        ts(R("opw"), R("qw"), R("pf", 3, 4), A.add)
         ts(R("k1"), R("qi"), -17.5, A.add, 1.0 / 36, A.mult)
         tt(R("k4"), R("qi"), R("gp"), A.add)
         copy("v", R("k2"), R("k1"))
         ts(R("k3"), R("k2"), 252.0, A.mult, R("pf", 7, 8), A.add)
         tt(R("k1"), R("k3"), R("k4"), A.add)
-        copy("v", R("tgt"), R("k1"))
+        copy("v", R("o1"), R("k1"))
+        offsets("tgt", look("st", 1, "o1"), max(me - 2, 0) % 2 == 0)
 
     def first_list():
         cuts = (0, 320, 608, 896, 4 * C)
@@ -360,51 +395,9 @@ def rank_program(g, core, T, topo):
         tt(R("nn"), R("tt"), na, A.add)
         tt(R("ee"), R("nn", 18, 36), R("nn", 0, 18), A.subtract)
         tt(R("ff"), R("ee"), R("cc"), A.mult)
-        for e in (0, 1):
-            tt(R("vv", 9 * e, 9 * e + 9), R("ff", e, 18, 2), R("nn", e, 18, 2), A.add)
-        copy("v", R("eb", 0, 72, 4), R("vv"))
-        copy("v", R("eb", 2, 72, 4), R("vv"))
-        tt(R("eb", 1, 72, 4), R("vv"), R("eb", 0, 72, 4), A.subtract)
-        tt(R("eb", 3, 72, 4), R("vv"), R("eb", 0, 72, 4), A.subtract)
-        k = 0
-        for q in range(4):
-            for a, c0, c1, b0 in ([(0, 0, 18, 1), (1, 0, 18, 19), (2, 0, 1, 37)] if q < 2 else
-                                  [(2, 0, 18, 1), (3, 0, 18, 19), (1, 17, 18, 0)]):
-                copy("vs"[k % 2], R("xin", 32 * b0, 32 * (b0 + c1 - c0), 8, 32 * q, 32 * q + 32),
-                     R("eb", 4 * c0, 4 * c1, 1, 32 * a, 32 * a + 32))
-                k += 1
-        turn(R("t0", HALF, HALF + OWN + 32), R("xin"))
-
-    def double(l):
-        new, old, off = "t%d" % (l % 2), "t%d" % (1 - l % 2), "of%d" % (1 - l % 2)
-        for e, a, b in (("v", 0, CUT), ("s", CUT, CUT2), ("s", CUT2, OWN)):
-            copy(e, R(new, HALF + a, HALF + b), R(old), R(off, a // 16, b // 16))
-
-    def swap_lo(l, e, a, b):
-        t = "t%d" % (l % 2)
-        copy(e, R(t, a, b, p0=64), R(t, HALF + a, HALF + b, p1=64))
-
-    def swap_hi(l, e, a, b):
-        t = "t%d" % (l % 2)
-        copy(e, R(t, HALF + OWN + a, HALF + OWN + b, p1=64), R(t, OWN + a, OWN + b, p0=64))
-
-    def wrap(l, swap=False):
-        t, w = "t%d" % (l % 2), 96 * l
-        if l == 0:
-            turn(R("y0"), R(t, HALF, HALF + OWN))
-            turn(R("y1"), R(t, HALF + 16, HALF + OWN + 16))
-            tt(R("wv", 0, 74, 2), R("y0", 0, OWN, 32), R("y0", 8, OWN, 32), A.add)
-            tt(R("wv", 1, 74, 2), R("y1", 0, OWN, 32), R("y1", 8, OWN, 32), A.add)
-        else:
-            for a, b in ((0, CUT), (CUT, CUT2), (CUT2, OWN)):
-                turn(R("y0", a, b), R(t, HALF + a, HALF + b))
-                if swap and b < OWN:
-                    swap_hi(l, "v", max(a - 32, 0), b - 32)
-            tt(R("wv", w, w + 74), R("y0", 0, OWN, 16), R("y0", 8, OWN, 16), A.add)
-        if l < 7:
-            ts(R("of%d" % (l % 2)), R("wv", w, w + 74), SH1 if l else SH0, A.add)
-        if swap:
-            swap_hi(l, "v", CUT2 - 32, HALF)
+        tt(R("vv"), R("ff"), R("nn", 0, 18), A.add)
+        offsets("of", R("vv"), False)
+        gather("oo", 0, "st", "of")
 
     def unpack(t, todo, n, engines):
         for i in range(min(n, len(todo))):
@@ -418,26 +411,24 @@ def rank_program(g, core, T, topo):
                     o, s = R(z, M * b + HALF, M * b + M, 1, p, p + 64), R(z, M * b, M * b + HALF, 1, 64 - p, 128 - p)
                     dma("y", "zx%d_%d" % (b, t), ap(o), ap(s), [s], [o])
 
-    def look(table, off):
-        copy("v", R("gs", 0, 128), R(table), R(off, 0, 8))
-        copy("s", R("gs", 128, C), R(table), R(off, 8, 18))
-        turn(R("ys"), R("gs"))
-        tt(R("v1"), R("ys", 0, C, 16), R("ys", 8, C, 16), A.add)
+    def ahead():
+        l = me - 2
+        offsets("o1", look(*table(l), "tgt"), l % 2 == 0)
+        offsets("o1", look(*table(l), "o1"), l % 2 == 1)
 
-    def places(l):
-        table = "t%d" % (l % 2)
-        look(table, "tgt")
-        if me:
-            ts(R("o1"), R("v1"), SH1 if l else SH0, A.add)
-            look(table, "o1")
+    def places():
+        if me == 1:
+            offsets("o1", look(*table(0), "tgt"), True)
+        lab = look(*table(max(me - 1, 0)), "o1" if me else "tgt")
         for k, w in enumerate((C, 36, 144)):
-            ts(R("ta", 18 * k, 18 * k + 18), R("v1"), -(32 + (w - 1) / 2.0), A.add, 1.0 / w, A.mult)
+            ts(R("ta", 18 * k, 18 * k + 18), lab, -4.0 * (w - 1), A.add, 0.125 / w, A.mult)
+        ts(R("v1"), lab, 0.125, A.mult, SHZ, A.add)
         copy("v", R("ti"), R("ta"))
         tt(R("tm"), R("ti"), R("co"), A.mult)
         tt(R("f1"), R("tm", 0, 18), R("tm", 18, 36), A.add)
         tt(R("f2"), R("tm", 36, 54), R("v1"), A.add)
         tt(R("f3"), R("f1"), R("f2"), A.add)
-        ts(R("oz"), R("f3"), SHZ, A.add)
+        copy("v", R("oz"), R("f3"))
 
     def serve(t):
         for b in range(4):
@@ -472,45 +463,51 @@ def rank_program(g, core, T, topo):
             else:
                 ts(out, src, 0.0, A.max, 0.03125, A.mult)
 
+    def own(l):
+        copy("s", R("pw", C * (l // 2), C * (l // 2) + C), R("tb"), R("opw"))
+
+    def lists_in():
+        a, b = R("pw", p0=1, p1=2), R("oo", 4 * C, 8 * C, 1, 16 * me + 1, 16 * me + 2)
+        dma("y", "pr", T.plt[0:4, :], ap(a), [a], [R("plt", p1=4)])
+        dma("y", "pr", T.plt[4:8, :], ap(b), [b], [R("plt", p0=4, p1=8)])
+
     def lists_out():
-        c0, p0 = 18 * (me % 4) + 2, 64 * (me // 4)
-        for l in range(8):
-            turn(R("plt", 32 * l, 32 * l + 32), R("wv", 96 * l + c0, 96 * l + c0 + 32))
-        ts(R("plo"), R("plt"), -32.0, A.add)
-        for l in range(8):
-            s = R("plo", 32 * l, 32 * l + 16, 1, p0, p0 + 18)
-            dma("y", "out", T.pl[l:l + 1, :], ap(s), [s], [])
+        ts(R("pli", p1=8), R("plt", p1=8), 0.125, A.mult)
+        copy("v", R("plo", p1=8), R("pli", p1=8))
+        for k in (0, 1):
+            s = R("plo", p0=4 * k, p1=4 * k + 4)
+            dma("y", "out", T.pl[k:8:2, :], ap(s), [s], [])
 
     dma("y", "lx", T.x0[:], T.x[:], [], [R("x0")])
     dma("s", "c0", T.dsc[me], T.sc[:], [], [slot("dsc", me)])
     dma("y", "lu", T.ub[:], T.u[:], [], [R("ub")])
-    iota(R("st", 0, 576), [[1, 576]], 32, 0)
+    iota(R("st", 0, C), [[256, 9], [129, 2], [8, 16]], 1, 0)
     iota(R("valm"), [[-64, 2], [0, 4], [-1, 16]], 0, 1)
     iota(R("pi", 0, 1), [[0, 1]], 0, 1)
     spread(T.dsc[me], [slot("dsc", me)], "ca")
     arrives("ca", N - 1, [slot("dsc", r) for r in others])
-    if me:
-        iota(R("qi"), [[16, 18]], 0, 0)
-        iota(R("gp"), [[0, 18]], 32, 0)
-    else:
+    if turned:
         iota(R("qi"), [[32, 9], [0, 2]], 0, 0)
-        iota(R("gp"), [[0, 9], [36, 2]], 32, 0)
+        iota(R("gp"), [[0, 9], [36, 2]], 0, 0)
+    else:
+        iota(R("qi"), [[16, 18]], 0, 0)
+        iota(R("gp"), [[0, 18]], 0, 0)
+    iota(R("qw"), [[32, 9], [C, 2]], 2 * C * (me // 2) + 16 * (me % 2), 0)
     iota(R("vale"), [[-32, 4], [256, 2], [-1, 16]], 0, 1)
     fill(R("srow", C, 384, p1=32), 0.0)
-    fill(R("xin"), 16.0)
-    plus(R("st", 576, HALF), R("st", 0, 576), 576.0)
-    plus(R("st", HALF, M), R("st", 0, HALF), float(HALF))
+    plus(R("st", C, 2 * C), R("st", 0, C), 8.0 * C - 1)
+    plus(R("st", 2 * C, HALF), R("st", 0, 2 * C), 16.0 * C)
+    plus(R("st", HALF, M), R("st", 0, HALF), 8.0 * HALF)
+    fill(R("tb", 0, HALF), 0.0)
 
     for t in range(ROUNDS):
         last = t == ROUNDS - 1
         parts_out(t)
         score(t)
         if t == 0:
-            for k in (0, 1):
-                copy("s", R("t%d" % k, 0, HALF, p1=64), R("xin", 0, HALF, p1=64))
-                copy("s", R("t%d" % k, HALF + OWN, TW, p0=64), R("xin", 0, HALF, p0=64))
             dma("y", "c1", T.o32[:], T.dsc[:], [slots("dsc")], [R("o32")])
             columns()
+            copy("s", R("tb", HALF, M), R("tb", 0, HALF))
             movers(0, "valm", [0, 16, 32, 48])
             for k, kk in enumerate((0, 2, 1, 3)):
                 copy("v", R("osc16", 18 * k, 18 * k + 18), R("o32", 18 * kk, 18 * kk + 18))
@@ -518,62 +515,48 @@ def rank_program(g, core, T, topo):
         score_rows(t)
         hop1(t)
         if t == 0:
-            wait("y", ("ha0", None))
-            dma("y", "lw", bits(R("wq")), T.wc[:], [], [R("wq")])
-            dma("y", "lw", T.wp[:], T.ws[:], [], [R("wp")])
-            dma("y", "lv", T.vb[:], T.v[:], [], [R("vb")])
+            wait("g", ("ha0", None))
+            dma("g", "lw", bits(R("wq")), T.wc[:], [], [R("wq")])
+            dma("g", "lw", T.wp[:], T.ws[:], [], [R("wp")])
+            dma("g", "lv", T.vb[:], T.v[:], [], [R("vb")])
             pad(0)
             pad(1)
         first_list()
         todo = list(range(16))
-        mine = max(me - 1, 0)
-        send = max(mine, 3) if last else mine
-        early = 1 if send < 5 else 2
-        for l in range(8 if last else mine + 1):
-            if l:
-                double(l)
-            if l < 7:
-                swap_lo(l, "g", 0, 256 if l == mine else CUT)
+        mine = max(me, 1)
+        top = 7 if last else mine - 1
+        sent = False
+        for l in range(max(top, mine) + 1):
+            late = l == 7 == me
+            if 0 < l <= top and not late:
+                gather("oo", rows(l)[0], table(l - 1)[0], "of")
+            if l <= min(top, 6):
+                lay(t, l)
+            if l == me - 1 and me >= 2:
+                ahead()
             if l == mine:
-                swap_hi(l, "v", 0, CUT - 32)
-                swap_lo(l, "s", CUT2, HALF)
-                swap_hi(l, "v", CUT - 32, CUT2 - 32)
-                swap_lo(l, "v", 256, CUT2)
-                swap_hi(l, "v", CUT2 - 32, HALF)
-                if l == send:
-                    unpack(t, todo, 16, "sv")
-                places(l)
-                if l == send:
-                    serve(t)
-                elif l >= early:
-                    unpack(t, todo, 8, "s")
-                if last:
-                    wrap(l)
-                continue
-            if l == 7:
-                wrap(l)
-            elif l == 0:
-                swap_lo(l, "s", CUT, HALF)
-                swap_hi(l, "s", 576, HALF)
-                wrap(l)
-                swap_hi(l, "v", 0, 576)
-            elif todo and l >= early:
-                unpack(t, todo, {6: 4, 5: 6, 4: 6}.get(send, 8), "s")
-                swap_lo(l, "g", CUT, 704)
-                wrap(l, True)
-                swap_lo(l, "v", 704, HALF)
-            else:
-                swap_lo(l, "s", CUT, HALF)
-                wrap(l, True)
-            if l == send:
+                places()
+            if l >= mine and not sent and (not todo or not last):
+                unpack(t, todo, 16, "sv")
                 serve(t)
+                sent = True
+            if late:
+                wrap(6)
+                gather("oo", rows(7)[0], table(6)[0], "of")
+            if l < top and not (l == 6 and me == 7):
+                wrap(l)
+            if last and l % 2:
+                own(l - 1)
+            if l >= 1:
+                unpack(t, todo, 4 if last or me >= 6 else 6, "s" if last or me >= 6 else "ssv")
         if t == 0:
             movers(4, "vale", [0, 256, 16, 272])
-            fill(R("wv"), 0.0)
             quant(R("vq"), R("vs"), R("vb"))
         if last:
-            lists_out()
+            lists_in()
         take(t, 0, 3)
+        if last:
+            lists_out()
         take(t, 3, 4)
         layer(t)
 

@@ -4,9 +4,22 @@ from concourse.mybir import dt, AluOpType, ActivationFunctionType
 N, C, ROUNDS = 8, 288, 2
 M = N * C
 HALF = M // 2
-PAD = 128 - 108
-TRADE = C - 16
+SIDE = 144 + 128
 Q4, U8, BF, F32, I32, U16 = "float8_e4m3fn_x4", "uint8", "bfloat16", "float32", "int32", "uint16"
+CHAIN = [[], [0, None], [None, 1, 0, 1], [0, 1, 2, 3], [0, 1, 0, 3, 2, 5], [0, 1, 0, 1, 4, 5, 4, 7],
+         [0, 1, 0, 3, 4, 3, 6, 7, 6, 7], [0, 1, 0, 3, 4, 3, 6, 7, 6, 7, 8, 9]]
+TRADE, PLAIN = ("st", 1), ("tb", 15)
+FROM = (3, 2)
+
+
+def homes(chain):
+    at = {None: TRADE}
+    reads = [None] + list(chain)
+    for s in sorted(set(chain) - {None}):
+        busy = {at[u][0] for u in reads[s:s + 2] if u in at}
+        name = [b for b in ("st", "tb", "tc") if b not in busy][0]
+        at[s] = (name, 3 + s)
+    return at
 
 
 def _sb(n, d):
@@ -17,37 +30,30 @@ SCRATCH = {
     "ub": _sb(512, BF), "vb": _sb(512, BF), "uq": _sb(128, Q4), "us": _sb(128, U8), "vq": _sb(128, Q4), "vs": _sb(128, U8),
     "wq": _sb(512, Q4), "wp": _sb(512, U8),
     "ct": _sb(8 * 516, BF), "mq": _sb(32 * 128, Q4), "ms": _sb(32 * 128, U8), "valm": _sb(128, F32), "vale": _sb(128, F32),
-    "st": _sb(M, F32), "tb": _sb(M, F32), "srow": _sb(384, F32), "sg": _sb(4 * C, F32), "sv": _sb(4 * C, F32),
-    "o32": _sb(72, I32), "osc16": _sb(72, U16),
+    "st": _sb(M, F32), "tb": _sb(M, F32), "tc": _sb(M, F32), "srow": _sb(384, F32), "sg": _sb(4 * C, F32), "sv": _sb(4 * C, F32),
+    "si": _sb(72, I32), "sf": _sb(128, F32), "sx": _sb(128, F32), "rb": _sb(C, F32), "rt": _sb(C, F32), "osc16": _sb(72, U16),
     "gt": _sb(36, F32), "mx": _sb(36, F32), "df": _sb(36, F32), "tt": _sb(36, F32), "nn": _sb(36, F32),
     "cc": _sb(18, F32), "ee": _sb(18, F32), "ff": _sb(18, F32), "vv": _sb(18, F32),
-    "oo": _sb(8 * C, F32), "y0": _sb(C, F32), "of": _sb(18, U16), "pw": _sb(4 * C, F32), "opw": _sb(18, U16),
-    "plt": _sb(C, F32), "pli": _sb(C, I32), "plo": _sb(C, F32),
-    "ci": _sb(18, I32), "cw": _sb(18, F32), "cx": _sb(18, F32), "cy": _sb(18, F32),
-    "pi": _sb(4, I32), "pf": _sb(8, F32), "qi": _sb(18, F32), "gp": _sb(18, F32), "k1": _sb(18, F32), "k2": _sb(18, I32),
-    "k3": _sb(18, F32), "k4": _sb(18, F32), "tgt": _sb(18, U16), "qw": _sb(18, F32),
-    "gs": _sb(C, F32), "ys": _sb(C, F32), "v1": _sb(18, F32), "o1": _sb(18, U16),
-    "ta": _sb(54, F32), "ti": _sb(54, I32), "tm": _sb(54, F32), "co": _sb(54, F32), "f1": _sb(18, F32), "f2": _sb(18, F32),
-    "f3": _sb(18, F32), "oz": _sb(18, U16), "yo": _sb(C, F32),
-    "dsc": ("dram", [N, 128, 9], I32),
+    "oo": _sb(8 * C, F32), "yy": _sb(2 * C, F32), "of": _sb(36, U16), "ow": _sb(18, U16), "oz": _sb(18, U16), "opl": _sb(18, U16),
+    "pf": _sb(1, F32), "pr": _sb(C, F32), "yo": _sb(C, F32), "z": _sb(4 * M + HALF, BF),
+    "dsc": ("dram", [N, 128, 9], F32), "dp": ("dram", [N, 128, 3], F32), "dq": ("dram", [N, 128, 3], F32),
 }
 for _t in range(ROUNDS + 1):
     SCRATCH.update({"x%d" % _t: _sb(4 * C, BF), "xq%d" % _t: _sb(C, Q4), "xs%d" % _t: _sb(C, U8)})
 for _t in range(ROUNDS):
     for _n in ("s", "g", "zp", "h"):
         SCRATCH["%sb%d" % (_n, _t)] = _sb(4 * C, BF)
-    for _n, _w in (("s", C), ("a", C), ("g", C), ("b", 2 * PAD + C), ("h", C), ("ra", 72), ("rb", 72)):
+    for _n, _w in (("s", C), ("a", C), ("g", C), ("b", 2 * SIDE), ("h", C), ("ra", 72), ("rb", 72)):
         SCRATCH["%sq%d" % (_n, _t)] = _sb(_w, Q4)
         SCRATCH["%ss%d" % (_n, _t)] = _sb(_w, U8)
-    SCRATCH["z%d" % _t] = _sb(4 * M, BF)
     SCRATCH["dx%d" % _t] = ("dram", [16, N, 4 * C], BF)
     SCRATCH["dl%d" % _t] = ("dram", [N, 128, 3], F32)
 for _b in range(8):
     SCRATCH["pb%d" % _b] = ("psum", [128, 512], F32)
 
-_PER_ROUND = (["so", "sa", "sr", "d1_", "d2_", "ha", "pd", "raq", "ras", "rbq", "rbs"]
-              + ["zx%d_" % _b for _b in range(4)] + ["hb%d_" % _r for _r in range(N)] + ["bc%d_" % _l for _l in range(7)])
-SEMAPHORES = (["cv", "cs", "cp", "cg", "sent", "lx", "lu", "lv", "lw", "c0", "ca", "c1", "out", "pr"]
+_PER_ROUND = (["so", "sa", "sr", "d1_", "d2_", "ha", "raq", "ras", "rbq", "rbs", "sb"]
+              + ["zx%d_" % _b for _b in range(4)] + ["hb%d_" % _r for _r in range(N)] + ["bc%d_" % _l for _l in range(11)])
+SEMAPHORES = (["cv", "cs", "cp", "cg", "sent", "lx", "lu", "lv", "lw", "ls", "c0", "ca", "c1", "nu", "out", "p0", "pa"]
               + ["%s%d" % (n, t) for t in range(ROUNDS) for n in _PER_ROUND])
 
 
@@ -62,7 +68,7 @@ def served(src, k):
 
 
 def landing(hop, src, t):
-    c0 = PAD + 36 * (src // 2) + (PAD + 144) * (src % 2) if hop == "b" else 36 * src
+    c0 = 36 * ((src // 2 + 1) % 4) + SIDE * (src % 2) if hop == "b" else 36 * src
     return hop + "q%d" % t, hop + "s%d" % t, c0, ("ha%d" % t if hop == "a" else "hb%d_%d" % (src, t))
 
 
@@ -183,14 +189,14 @@ def rank_program(g, core, T, topo):
     others = [r for r in range(N) if r != me]
     relays = relays_of(core, topo)
 
-    def remote(ts, n, reads):
-        order("g", reads, [])
-        g.remote_dma_fused(ts, local_sem=T.sem.sent)
-        more("sent", n)
-        note("g", ("sent", None), reads, [])
+    def remote(ts, n, reads, left="sent"):
+        order("g", reads, [], own=left)
+        g.remote_dma_fused(ts, local_sem=T.sem[left])
+        more(left, n)
+        note("g", (left, None), reads, [])
 
-    def spread(piece, reads, sem):
-        remote([transfer(topo, core, T.cores[r], [topo.engines(core, T.cores[r])[i]], T.sem[sem], piece, piece)
+    def spread(piece, to, reads, sem):
+        remote([transfer(topo, core, T.cores[r], [topo.engines(core, T.cores[r])[i]], T.sem[sem], piece(r), to)
                 for i, r in enumerate(others)], len(others), reads)
 
     def arrives(sem, n, writes):
@@ -236,22 +242,21 @@ def rank_program(g, core, T, topo):
         return R("mq", 128 * k, 128 * k + 128), R("ms", 128 * k, 128 * k + 128)
 
     def iota(out, pattern, base, cm):
-        if SCRATCH[out[0]][2] != I32:
-            op("g", lambda: g.iota(ap(out), pattern, base, cm, allow_small_or_imprecise_dtypes=True), [], [out])
-        else:
-            op("g", lambda: g.iota(ap(out), pattern, base, cm), [], [out])
+        op("g", lambda: g.iota(ap(out), pattern, base, cm, allow_small_or_imprecise_dtypes=True), [], [out])
 
     def plus(out, in_, c):
         op("s", lambda: g.scalar.activation(ap(out), ap(in_), ACT.Identity, bias=c), [in_], [out])
+
+    def grow(name, first):
+        for k, c in enumerate(first):
+            w = C << k
+            plus(R(name, w, 2 * w), R(name, 0, w), float(c))
 
     def slot(name, k):
         return (name, 0, 128, k, k + 1, 1)
 
     def slots(name):
         return (name, 0, 128, 0, N, 1)
-
-    SHZ = R("pf", 6, 7)
-    turned = me == 1
 
     def parts_out(t):
         for k in range(N):
@@ -260,7 +265,6 @@ def rank_program(g, core, T, topo):
                 [] if t == 0 else [R("x%d" % t, p0=16 * k, p1=16 * k + 16)], [slot("dx%d" % t, k)])
 
     def parts_in(t):
-        wait("y", ("so%d" % t, None))
         for d in range(N):
             dma("y", "d2_%d" % t, T["sb%d" % t][16 * d:16 * d + 16, :], T["dx%d" % t][:, :, 144 * d:144 * d + 144],
                 [slots("dx%d" % t)], [R("sb%d" % t, p0=16 * d, p1=16 * d + 16)])
@@ -271,7 +275,8 @@ def rank_program(g, core, T, topo):
             to = "r%s%s%d" % (name, kind, t)
             engs = [share(topo.engines(core, c), k, 4) for k, c in enumerate(relays)]
             remote([transfer(topo, core, c, engs[k], T.sem[to], view(R(buf, 72 * k, 72 * k + 72)), view(R(to)))
-                    for k, c in enumerate(relays)], sum(len(e) for e in engs), [R(buf)])
+                    for k, c in enumerate(relays)], sum(len(e) for e in engs), [R(buf)],
+                   "sb%d" % t if name == "b" else "sent")
         lq, ls, c0, sem = landing(name, me, t)
         a, b = R(sq, 36 * me, 36 * me + 36), R(ss, 36 * me, 36 * me + 36)
         dma("y", sem, bits(R(lq, c0, c0 + 36)), bits(a), [a], [R(lq, c0, c0 + 36)])
@@ -288,10 +293,10 @@ def rank_program(g, core, T, topo):
         if t == 0:
             quant(R("uq"), R("us"), R("ub"))
         mm(7, R("uq"), R("us"), xq, xs)
-        copy("s", R("srow", 0, C, p1=1), R("pb7", 0, C, p1=1))
+        copy("v", R("srow", 0, C, p1=1), R("pb7", 0, C, p1=1))
         dl = "dl%d" % t
-        dma("s", "so%d" % t, T[dl][me], T.srow[0:1, :], [R("srow", p1=1)], [slot(dl, me)])
-        spread(T[dl][me], [slot(dl, me)], "sa%d" % t)
+        dma("y", "so%d" % t, T[dl][me], T.srow[0:1, :], [R("srow", p1=1)], [slot(dl, me)])
+        spread(lambda r: T[dl][me], T[dl][me], [slot(dl, me)], "sa%d" % t)
         arrives("sa%d" % t, N - 1, [slot(dl, r) for r in others])
 
     def score_rows(t):
@@ -301,14 +306,8 @@ def rank_program(g, core, T, topo):
 
     def hop1(t):
         quant(R("sq%d" % t), R("ss%d" % t), R("sb%d" % t))
-        wait("g", ("sr%d" % t, None))
+        wait("g", ("sa%d" % t, None))
         hop("s", "a", t)
-
-    def pad(t):
-        a, b = R("xq0", 0, PAD), R("xs0", 0, PAD)
-        for c in (0, PAD + 144):
-            dma("g", "pd%d" % t, bits(R("bq%d" % t, c, c + PAD)), bits(a), [a], [R("bq%d" % t, c, c + PAD)])
-            dma("g", "pd%d" % t, ap(R("bs%d" % t, c, c + PAD)), ap(b), [b], [R("bs%d" % t, c, c + PAD)])
 
     def movers(first, src, wanted):
         fill(R("ct", 516 * first, 516 * first + 4 * 516), 0.0)
@@ -319,65 +318,30 @@ def rank_program(g, core, T, topo):
             o = 516 * (k // 4) + 3 - k % 4
             quant(*const(k), R("ct", o, o + 512))
 
-    def table(l):
-        return ("st", 2) if l % 2 else ("tb", 1)
+    def successors_out():
+        fill(R("sf", p1=32), 0.0)
+        for k in range(4):
+            copy("v", R("sf", 32 * k, 32 * k + 18, p1=16), R("si", 18 * k, 18 * k + 18, p1=16))
+        turn(R("sx", p1=32), R("sf", p1=32))
+        for k in range(4):
+            s = R("sx", 32 * k, 32 * k + 16, p1=18)
+            dma("ys"[k % 2], "c0", T.dsc[me, 32 * k:32 * k + 32, :], ap(s), [s], [slot("dsc", me)])
+        spread(lambda r: T.dsc[me], T.dsc[me], [slot("dsc", me)], "ca")
+        arrives("ca", N - 1, [slot("dsc", r) for r in others])
 
-    def rows(l):
-        c0 = C * (l // 2 + 4 * (l % 2))
-        return c0, (table(l - 1)[1] if l else 1)
+    def successors_in():
+        for r in range(N):
+            for k in range(4):
+                dma("ys"[k % 2], "c1", T.rb[k:128:16, 36 * r:36 * r + 36], T.dsc[r, 32 * k:32 * k + 32, :],
+                    [slots("dsc")], [R("rb", 36 * r, 36 * r + 36)])
 
-    def gather(out, c0, src, off):
-        copy("v", R(out, c0, c0 + 128), R(src), R(off, 0, 8))
-        copy("s", R(out, c0 + 128, c0 + C), R(src), R(off, 8, 18))
+    def successor_offsets():
+        turn(R("rt"), R("rb"))
+        for k, kk in enumerate((0, 2, 1, 3)):
+            copy("v", R("osc16", 18 * k, 18 * k + 18), R("rt", kk, C, 16))
 
-    def offsets(out, labels, traded):
-        if not traded:
-            ts(R(out), labels, 0.125, A.mult)
-            return
-        ts(R("ci"), labels, 0.125, A.mult)
-        ts(R("cw"), labels, float(TRADE), A.mult, -float(TRADE), A.add)
-        ts(R("cx"), R("ci"), 1.0 - 8 * TRADE, A.mult)
-        tt(R("cy"), R("cw"), R("cx"), A.add)
-        copy("v", R(out), R("cy"))
-
-    def lay(t, l):
-        c0, row = rows(l)
-        name, to = table(l)
-        for d in range(8):
-            dma("ys"[d % 2], "bc%d_%d" % (l, t), T[name][16 * d + to:16 * d + to + 1, :], T.oo[row:128:16, c0:c0 + C],
-                [R("oo", c0, c0 + C)], [R(name, p0=16 * d + to, p1=16 * d + to + 1)])
-
-    def wrap(l):
-        c0, row = rows(l)
-        turn(R("y0"), R("oo", c0, c0 + C))
-        offsets("of", R("y0", row, C, 16), l % 2 == 0)
-
-    def look(src, row, off):
-        gather("gs", 0, src, off)
-        turn(R("ys"), R("gs"))
-        return R("ys", row, C, 16)
-
-    def columns():
-        for p0, lo in ((0, True), (64, False)):
-            fill(R("pf", 6, 7, p0=p0, p1=p0 + 64), 0.0 if lo else float(HALF))
-            fill(R("co", 0, 18, p0=p0, p1=p0 + 64), -9 * 252.0 if lo else 2 * M - 9 * 252.0)
-            fill(R("co", 36, 54, p0=p0, p1=p0 + 64), 0.0 if lo else -float(M))
-        fill(R("co", 18, 36), 252.0)
-        sh = 5 if turned else 4
-        ts(R("pi", 1, 2), R("pi", 0, 1), (1 << sh) - 1, A.bitwise_and)
-        ts(R("pi", 2, 3), R("pi", 0, 1), sh, A.arith_shift_right)
-        ts(R("pi", 3, 4), R("pi", 0, 1), 15, A.bitwise_and)
-        copy("v", R("pf", 0, 4), R("pi"))
-        ts(R("pf", 7, 8), R("pf", 2, 3), 72.0 if turned else 36.0, A.mult)
-        ts(R("qi"), R("qi"), R("pf", 1, 2), A.add)
-        ts(R("opw"), R("qw"), R("pf", 3, 4), A.add)
-        ts(R("k1"), R("qi"), -17.5, A.add, 1.0 / 36, A.mult)
-        tt(R("k4"), R("qi"), R("gp"), A.add)
-        copy("v", R("k2"), R("k1"))
-        ts(R("k3"), R("k2"), 252.0, A.mult, R("pf", 7, 8), A.add)
-        tt(R("k1"), R("k3"), R("k4"), A.add)
-        copy("v", R("o1"), R("k1"))
-        offsets("tgt", look("st", 1, "o1"), max(me - 2, 0) % 2 == 0)
+    chain = CHAIN[me]
+    home = homes(chain)
 
     def first_list():
         cuts = (0, 320, 608, 896, 4 * C)
@@ -386,7 +350,7 @@ def rank_program(g, core, T, topo):
         for i in range(4):
             turn(R("sv", cuts[i], cuts[i + 1]), R("sg", cuts[i], cuts[i + 1]))
         sa, sb = R("sv", 0, 576, 16), R("sv", 576, 1152, 16)
-        na, nb = R("sv", 1, 576, 16), R("sv", 577, 1152, 16)
+        na, nb = R("sv", 2, 576, 16), R("sv", 578, 1152, 16)
         tt(R("gt"), sb, sa, A.is_gt)
         tt(R("df"), nb, na, A.subtract)
         tt(R("mx"), sb, sa, A.max)
@@ -396,57 +360,89 @@ def rank_program(g, core, T, topo):
         tt(R("ee"), R("nn", 18, 36), R("nn", 0, 18), A.subtract)
         tt(R("ff"), R("ee"), R("cc"), A.mult)
         tt(R("vv"), R("ff"), R("nn", 0, 18), A.add)
-        offsets("of", R("vv"), False)
-        gather("oo", 0, "st", "of")
+        copy("v", R("ow"), R("vv"))
 
-    def unpack(t, todo, n, engines):
-        for i in range(min(n, len(todo))):
+    def step(t, i, table, off, o0):
+        name, row = home[table]
+        c0 = C * (i % 8)
+        copy("v", R("oo", c0, c0 + 128), R(name), R(off, o0, o0 + 8))
+        copy("s", R("oo", c0 + 128, c0 + C), R(name), R(off, o0 + 8, o0 + 18))
+        if i in home:
+            to, at = home[i]
+            for d in range(8):
+                dma("ys"[d % 2], "bc%d_%d" % (i, t), T[to][16 * d + at:16 * d + at + 1, :], T.oo[row:128:16, c0:c0 + C],
+                    [R("oo", c0, c0 + C)], [R(to, p0=16 * d + at, p1=16 * d + at + 1)])
+        return c0, row
+
+    def wrap(i, c0, row, offsets=True):
+        y0 = C * (i % 2)
+        turn(R("yy", y0, y0 + 128), R("oo", c0, c0 + 128))
+        turn(R("yy", y0 + 128, y0 + C), R("oo", c0 + 128, c0 + C))
+        if offsets:
+            o0 = 18 * (i % 2)
+            copy("v", R("of", o0, o0 + 8), R("yy", y0 + row, y0 + 128, 16))
+            copy("v", R("of", o0 + 8, o0 + 18), R("yy", y0 + 128 + row, y0 + C, 16))
+        return R("yy", y0 + row, y0 + C, 16)
+
+    def unpack(t, todo, engines):
+        for e in engines[:len(todo)]:
             j = todo.pop(0)
             b, d = j // 4, j % 4
-            z = "z%d" % t
+            own = M * b + HALF
             mm(j % 7, *const(4 * d + b), R("aq%d" % t), R("as%d" % t))
-            copy(engines[i % len(engines)], R(z, M * b + C * d, M * b + C * d + C), R("pb%d" % (j % 7), 0, C))
+            copy(e, R("z", own + C * d, own + C * d + C), R("pb%d" % (j % 7), 0, C))
             if d == 3:
-                for p in (0, 64):
-                    o, s = R(z, M * b + HALF, M * b + M, 1, p, p + 64), R(z, M * b, M * b + HALF, 1, 64 - p, 128 - p)
+                for p, c in ((0, own + HALF), (64, own - HALF)):
+                    o, s = R("z", c, c + HALF, 1, p, p + 64), R("z", own, own + HALF, 1, 64 - p, 128 - p)
                     dma("y", "zx%d_%d" % (b, t), ap(o), ap(s), [s], [o])
 
-    def ahead():
-        l = me - 2
-        offsets("o1", look(*table(l), "tgt"), l % 2 == 0)
-        offsets("o1", look(*table(l), "o1"), l % 2 == 1)
-
-    def places():
-        if me == 1:
-            offsets("o1", look(*table(0), "tgt"), True)
-        lab = look(*table(max(me - 1, 0)), "o1" if me else "tgt")
-        for k, w in enumerate((C, 36, 144)):
-            ts(R("ta", 18 * k, 18 * k + 18), lab, -4.0 * (w - 1), A.add, 0.125 / w, A.mult)
-        ts(R("v1"), lab, 0.125, A.mult, SHZ, A.add)
-        copy("v", R("ti"), R("ta"))
-        tt(R("tm"), R("ti"), R("co"), A.mult)
-        tt(R("f1"), R("tm", 0, 18), R("tm", 18, 36), A.add)
-        tt(R("f2"), R("tm", 36, 54), R("v1"), A.add)
-        tt(R("f3"), R("f1"), R("f2"), A.add)
-        copy("v", R("oz"), R("f3"))
+    def lists(t):
+        todo = list(range(16))
+        got = R("vv")
+        if chain:
+            wrap(0, *step(t, 0, None, "ow", 0))
+            if 1 in home:
+                step(t, 1, None, "of", 0)
+        for k, s in enumerate(chain):
+            i = k + 2
+            at = step(t, i, s, *(("ow", 0) if k == 0 else ("of", 18 * (k % 2 == 0))))
+            if k >= FROM[t]:
+                unpack(t, todo, "ss")
+            got = wrap(i, *at, offsets=k + 1 < len(chain))
+            if k >= FROM[t] and chain[k + 1:k + 2] == [k + 1] and s != k:
+                unpack(t, todo, "vvv")
+        ts(R("oz"), got, R("pf"), A.add)
+        unpack(t, todo, "sv" * 8)
+        return got
 
     def serve(t):
         for b in range(4):
-            copy("sv"[b % 2], R("gb%d" % t, b, 4 * C, 4), R("z%d" % t, M * b, M * b + M), R("oz"))
+            copy("sv"[b % 2], R("gb%d" % t, b, 4 * C, 4), R("z", M * b, M * b + M + HALF), R("oz"))
         quant(R("gq%d" % t), R("gs%d" % t), R("gb%d" % t))
         hop("g", "b", t)
+
+    def lists_out(got):
+        name, row = PLAIN
+        copy("v", R("opl"), got)
+        copy("s", R("pr"), R(name), R("opl"))
+        for r in range(N):
+            s = R("pr", 36 * r, 36 * r + 36)
+            to, sem = ("dq", "pa") if r == me else ("dp", "p0")
+            dma("s", sem, T[to][r, 0:96, :], T.pr[row:128:16, 36 * r:36 * r + 36], [s], [slot(to, r)])
+        spread(lambda r: T.dp[r], T.dq[me], [slots("dp")], "pa")
+        arrives("pa", N - 1, [slot("dq", r) for r in others])
 
     def take(t, k0, k1):
         zp, h = "zpb%d" % t, "hb%d" % t
         for f in (0, 1):
-            c1 = PAD + (PAD + 144) * f + 36 * k1
+            c0 = landing("b", 2 * k0 + f, t)[2]
             for i in range(8):
-                mm(i, *const(16 + 4 * (2 * (i // 4) + f) + i % 4), R("bq%d" % t, c1 - 128, c1), R("bs%d" % t, c1 - 128, c1),
+                mm(i, *const(16 + 4 * (2 * (i // 4) + f) + i % 4), R("bq%d" % t, c0, c0 + 128), R("bs%d" % t, c0, c0 + 128),
                    f == 0, f == 1)
         for i in range(8):
             e, b = i // 4, i % 4
             for k in range(k0, k1):
-                o = 128 - 36 * (k1 - k)
+                o = 36 * (k - k0)
                 copy("vs"[i % 2], R(zp, C * k + 144 * e + b, C * k + 144 * e + 144, 4), R("pb%d" % i, o, o + 36))
         for k in range(k0, k1):
             for a in range(4):
@@ -463,100 +459,60 @@ def rank_program(g, core, T, topo):
             else:
                 ts(out, src, 0.0, A.max, 0.03125, A.mult)
 
-    def own(l):
-        copy("s", R("pw", C * (l // 2), C * (l // 2) + C), R("tb"), R("opw"))
-
-    def lists_in():
-        a, b = R("pw", p0=1, p1=2), R("oo", 4 * C, 8 * C, 1, 16 * me + 1, 16 * me + 2)
-        dma("y", "pr", T.plt[0:4, :], ap(a), [a], [R("plt", p1=4)])
-        dma("y", "pr", T.plt[4:8, :], ap(b), [b], [R("plt", p0=4, p1=8)])
-
-    def lists_out():
-        ts(R("pli", p1=8), R("plt", p1=8), 0.125, A.mult)
-        copy("v", R("plo", p1=8), R("pli", p1=8))
-        for k in (0, 1):
-            s = R("plo", p0=4 * k, p1=4 * k + 4)
-            dma("y", "out", T.pl[k:8:2, :], ap(s), [s], [])
-
+    dma("s", "ls", T.si[0:16, :], T.sc[:], [], [R("si", p1=16)])
     dma("y", "lx", T.x0[:], T.x[:], [], [R("x0")])
-    dma("s", "c0", T.dsc[me], T.sc[:], [], [slot("dsc", me)])
     dma("y", "lu", T.ub[:], T.u[:], [], [R("ub")])
-    iota(R("st", 0, C), [[256, 9], [129, 2], [8, 16]], 1, 0)
+    iota(R("st", 0, C), [[32, 9], [C, 2], [1, 16]], 0, 0)
+    iota(R("tb", 0, C), [[C, 8], [1, 36]], 0, 0)
     iota(R("valm"), [[-64, 2], [0, 4], [-1, 16]], 0, 1)
-    iota(R("pi", 0, 1), [[0, 1]], 0, 1)
-    spread(T.dsc[me], [slot("dsc", me)], "ca")
-    arrives("ca", N - 1, [slot("dsc", r) for r in others])
-    if turned:
-        iota(R("qi"), [[32, 9], [0, 2]], 0, 0)
-        iota(R("gp"), [[0, 9], [36, 2]], 0, 0)
-    else:
-        iota(R("qi"), [[16, 18]], 0, 0)
-        iota(R("gp"), [[0, 18]], 0, 0)
-    iota(R("qw"), [[32, 9], [C, 2]], 2 * C * (me // 2) + 16 * (me % 2), 0)
-    iota(R("vale"), [[-32, 4], [256, 2], [-1, 16]], 0, 1)
     fill(R("srow", C, 384, p1=32), 0.0)
-    plus(R("st", C, 2 * C), R("st", 0, C), 8.0 * C - 1)
-    plus(R("st", 2 * C, HALF), R("st", 0, 2 * C), 16.0 * C)
-    plus(R("st", HALF, M), R("st", 0, HALF), 8.0 * HALF)
-    fill(R("tb", 0, HALF), 0.0)
+    fill(R("rb"), 0.0)
+    fill(R("pf", p1=64), float(HALF))
+    fill(R("pf", p0=64), 0.0)
+    fill(R("z", 0, HALF, p1=64), 0.0)
+    parts_out(0)
+    successors_out()
+    grow("st", (16, 2 * C, 4 * C))
 
     for t in range(ROUNDS):
         last = t == ROUNDS - 1
-        parts_out(t)
+        if t:
+            parts_out(t)
         score(t)
         if t == 0:
-            dma("y", "c1", T.o32[:], T.dsc[:], [slots("dsc")], [R("o32")])
-            columns()
-            copy("s", R("tb", HALF, M), R("tb", 0, HALF))
+            grow("tb", (36, 72, 144))
+            dma("s", "nu", T.st[2:128:16, :], T.tb[2:128:16, :], [R("tb")], [R("st")])
             movers(0, "valm", [0, 16, 32, 48])
-            for k, kk in enumerate((0, 2, 1, 3)):
-                copy("v", R("osc16", 18 * k, 18 * k + 18), R("o32", 18 * kk, 18 * kk + 18))
+            fill(R("z", 4 * M, 4 * M + HALF, p0=64), 0.0)
         parts_in(t)
+        if t == 0:
+            successors_in()
         score_rows(t)
         hop1(t)
         if t == 0:
-            wait("g", ("ha0", None))
-            dma("g", "lw", bits(R("wq")), T.wc[:], [], [R("wq")])
-            dma("g", "lw", T.wp[:], T.ws[:], [], [R("wp")])
-            dma("g", "lv", T.vb[:], T.v[:], [], [R("vb")])
-            pad(0)
-            pad(1)
+            successor_offsets()
+            iota(R("vale"), [[-32, 4], [256, 2], [-1, 16]], 0, 1)
+            if any(h[0] == "tc" for h in home.values()):
+                iota(R("tc"), [[0, M]], 0, 0)
         first_list()
-        todo = list(range(16))
-        mine = max(me, 1)
-        top = 7 if last else mine - 1
-        sent = False
-        for l in range(max(top, mine) + 1):
-            late = l == 7 == me
-            if 0 < l <= top and not late:
-                gather("oo", rows(l)[0], table(l - 1)[0], "of")
-            if l <= min(top, 6):
-                lay(t, l)
-            if l == me - 1 and me >= 2:
-                ahead()
-            if l == mine:
-                places()
-            if l >= mine and not sent and (not todo or not last):
-                unpack(t, todo, 16, "sv")
-                serve(t)
-                sent = True
-            if late:
-                wrap(6)
-                gather("oo", rows(7)[0], table(6)[0], "of")
-            if l < top and not (l == 6 and me == 7):
-                wrap(l)
-            if last and l % 2:
-                own(l - 1)
-            if l >= 1:
-                unpack(t, todo, 4 if last or me >= 6 else 6, "s" if last or me >= 6 else "ssv")
-        if t == 0:
-            movers(4, "vale", [0, 256, 16, 272])
-            quant(R("vq"), R("vs"), R("vb"))
+        got = lists(t)
+        serve(t)
         if last:
-            lists_in()
+            lists_out(got)
+        if t == 0:
+            wait("y", ("sb0", None))
+            dma("y", "lw", bits(R("wq")), T.wc[:], [], [R("wq")])
+            dma("y", "lw", T.wp[:], T.ws[:], [], [R("wp")])
+            dma("y", "lv", T.vb[:], T.v[:], [], [R("vb")])
+            dma("y", "p0", T.dp[:, 96:128, :], T.srow[0:N, C:384], [R("srow", C, 384, p1=N)], [slots("dp")])
+            for u in range(ROUNDS):
+                for c in (144, SIDE + 144):
+                    quant(R("bq%d" % u, c, c + 128), R("bs%d" % u, c, c + 128), R("x0", 0, 512))
+            movers(4, "vale", [0, 256, 16, 272])
         take(t, 0, 3)
         if last:
-            lists_out()
+            quant(R("vq"), R("vs"), R("vb"))
+            dma("y", "out", T.pl[:], T.dq[:, 0:96, :], [slots("dq")], [])
         take(t, 3, 4)
         layer(t)
 

@@ -5,11 +5,12 @@ N, C, ROUNDS = 8, 288, 2
 M = N * C
 HALF = M // 2
 SIDE = 144 + 128
+FILLER = 112
 Q4, U8, BF, F32, I32, U16 = "float8_e4m3fn_x4", "uint8", "bfloat16", "float32", "int32", "uint16"
-CHAIN = [[], [0, None], [None, 1, 0, 1], [0, 1, 2, 3], [0, 1, 0, 3, 2, 5], [0, 1, 0, 1, 4, 5, 4, 7],
-         [0, 1, 0, 3, 4, 3, 6, 7, 6, 7], [0, 1, 0, 3, 4, 3, 6, 7, 6, 7, 8, 9]]
+CHAIN = [[], [0, None], [None, 1, 0, 1], [0, 1, 2, 3], [0, None, 2, 3, 4, 5], [0, 1, 2, 3, 5, 6],
+         [0, 2, 3, 4, 5, 6], [0, 1, 2, 3, 5, 6, 7, 8]]
 TRADE, PLAIN = ("st", 1), ("tb", 15)
-FROM = (3, 2)
+FROM = [(2, 1)] * 6 + [(1, 1), (2, 2)]
 
 
 def homes(chain):
@@ -17,8 +18,7 @@ def homes(chain):
     reads = [None] + list(chain)
     for s in sorted(set(chain) - {None}):
         busy = {at[u][0] for u in reads[s:s + 2] if u in at}
-        name = [b for b in ("st", "tb", "tc") if b not in busy][0]
-        at[s] = (name, 3 + s)
+        at[s] = ([b for b in ("st", "tb") if b not in busy][0], 3 + s)
     return at
 
 
@@ -30,10 +30,11 @@ SCRATCH = {
     "ub": _sb(512, BF), "vb": _sb(512, BF), "uq": _sb(128, Q4), "us": _sb(128, U8), "vq": _sb(128, Q4), "vs": _sb(128, U8),
     "wq": _sb(512, Q4), "wp": _sb(512, U8),
     "ct": _sb(8 * 516, BF), "mq": _sb(32 * 128, Q4), "ms": _sb(32 * 128, U8), "valm": _sb(128, F32), "vale": _sb(128, F32),
-    "st": _sb(M, F32), "tb": _sb(M, F32), "tc": _sb(M, F32), "srow": _sb(384, F32), "sg": _sb(4 * C, F32), "sv": _sb(4 * C, F32),
+    "st": _sb(M, F32), "tb": _sb(M, F32), "srow": _sb(384, F32), "sg": _sb(4 * C, F32), "sv": _sb(4 * C, F32),
     "si": _sb(72, I32), "sf": _sb(128, F32), "sx": _sb(128, F32), "rb": _sb(C, F32), "rt": _sb(C, F32), "osc16": _sb(72, U16),
     "gt": _sb(36, F32), "mx": _sb(36, F32), "df": _sb(36, F32), "tt": _sb(36, F32), "nn": _sb(36, F32),
-    "cc": _sb(18, F32), "ee": _sb(18, F32), "ff": _sb(18, F32), "vv": _sb(18, F32),
+    "cc": _sb(36, F32), "ee": _sb(36, F32), "vv": _sb(18, F32),
+    "ci": _sb(18, I32), "cw": _sb(18, F32), "cx": _sb(18, F32), "cy": _sb(18, F32),
     "oo": _sb(8 * C, F32), "yy": _sb(2 * C, F32), "of": _sb(36, U16), "ow": _sb(18, U16), "oz": _sb(18, U16), "opl": _sb(18, U16),
     "pf": _sb(1, F32), "pr": _sb(C, F32), "yo": _sb(C, F32), "z": _sb(4 * M + HALF, BF),
     "dsc": ("dram", [N, 128, 9], F32), "dp": ("dram", [N, 128, 3], F32), "dq": ("dram", [N, 128, 3], F32),
@@ -43,7 +44,7 @@ for _t in range(ROUNDS + 1):
 for _t in range(ROUNDS):
     for _n in ("s", "g", "zp", "h"):
         SCRATCH["%sb%d" % (_n, _t)] = _sb(4 * C, BF)
-    for _n, _w in (("s", C), ("a", C), ("g", C), ("b", 2 * SIDE), ("h", C), ("ra", 72), ("rb", 72)):
+    for _n, _w in (("s", C), ("a", C), ("g", C), ("b", 2 * SIDE + 4), ("h", C), ("ra", 72), ("rb", 72)):
         SCRATCH["%sq%d" % (_n, _t)] = _sb(_w, Q4)
         SCRATCH["%ss%d" % (_n, _t)] = _sb(_w, U8)
     SCRATCH["dx%d" % _t] = ("dram", [16, N, 4 * C], BF)
@@ -52,15 +53,16 @@ for _b in range(8):
     SCRATCH["pb%d" % _b] = ("psum", [128, 512], F32)
 
 _PER_ROUND = (["so", "sa", "sr", "d1_", "d2_", "ha", "raq", "ras", "rbq", "rbs", "sb"]
-              + ["zx%d_" % _b for _b in range(4)] + ["hb%d_" % _r for _r in range(N)] + ["bc%d_" % _l for _l in range(11)])
+              + ["zx%d_" % _b for _b in range(4)] + ["hb%d_" % _r for _r in range(N)] + ["bc%d_" % _l for _l in range(9)])
 SEMAPHORES = (["cv", "cs", "cp", "cg", "sent", "lx", "lu", "lv", "lw", "ls", "c0", "ca", "c1", "nu", "out", "p0", "pa"]
               + ["%s%d" % (n, t) for t in range(ROUNDS) for n in _PER_ROUND])
 
 
-def relays_of(core, topo):
+def relays_of(T, r, topo):
+    core = T.cores[r]
     same = [c for c in topo.cores_of(core) if c != core and topo.die(c) == topo.die(core)]
     other = [c for c in topo.cores_of(core) if topo.die(c) != topo.die(core)]
-    return [same[0], other[0], same[1], other[1]]
+    return [(same, other)[(k + r) % 2][k // 2] for k in range(4)]
 
 
 def served(src, k):
@@ -68,7 +70,7 @@ def served(src, k):
 
 
 def landing(hop, src, t):
-    c0 = 36 * ((src // 2 + 1) % 4) + SIDE * (src % 2) if hop == "b" else 36 * src
+    c0 = FILLER + (-72, -36, 128, -108)[src // 2] + SIDE * (src % 2) if hop == "b" else 36 * src
     return hop + "q%d" % t, hop + "s%d" % t, c0, ("ha%d" % t if hop == "a" else "hb%d_%d" % (src, t))
 
 
@@ -109,8 +111,8 @@ def rank_program(g, core, T, topo):
     me = T.rank_of(core)
     if me is None:
         for r in range(N):
-            if core in relays_of(T.cores[r], topo):
-                relay_program(g, core, T, topo, r, relays_of(T.cores[r], topo).index(core))
+            if core in relays_of(T, r, topo):
+                relay_program(g, core, T, topo, r, relays_of(T, r, topo).index(core))
         return
     A, ACT = AluOpType, ActivationFunctionType
     queue = {"v": g.vector, "s": g.scalar, "p": g.tensor, "g": g, "y": g.sync}
@@ -187,7 +189,7 @@ def rank_program(g, core, T, topo):
         return ap(r).bitcast(dt.uint8)
 
     others = [r for r in range(N) if r != me]
-    relays = relays_of(core, topo)
+    relays = relays_of(T, me, topo)
 
     def remote(ts, n, reads, left="sent"):
         order("g", reads, [], own=left)
@@ -283,17 +285,24 @@ def rank_program(g, core, T, topo):
         dma("y", sem, ap(R(ls, c0, c0 + 36)), ap(b), [b], [R(ls, c0, c0 + 36)])
         for r in others:
             lq, ls, c0, sem = landing(name, r, t)
-            via = relays_of(T.cores[r], topo)[me // 2]
+            via = relays_of(T, r, topo)[me // 2]
             arrives(sem, 2 * len(share(topo.engines(via, core), 0, len(served(r, me // 2)))),
                     [R(lq, c0, c0 + 36), R(ls, c0, c0 + 36)])
 
-    def score(t):
-        xq, xs = R("xq%d" % t), R("xs%d" % t)
-        quant(xq, xs, R("x%d" % t))
-        if t == 0:
+    def product(t, c):
+        xq, xs = R("xq%d" % t, c, c + 144), R("xs%d" % t, c, c + 144)
+        quant(xq, xs, R("x%d" % t, 4 * c, 4 * c + 576))
+        if t == 0 and c == 0:
             quant(R("uq"), R("us"), R("ub"))
-        mm(7, R("uq"), R("us"), xq, xs)
-        copy("v", R("srow", 0, C, p1=1), R("pb7", 0, C, p1=1))
+        w = "v" if t == ROUNDS else "u"
+        mm(c // 36, R(w + "q"), R(w + "s"), xq, xs)
+
+    def score(t):
+        if t == 0:
+            product(0, 0)
+            product(0, 144)
+        for c in (0, 144):
+            copy("s" if t and not c else "v", R("srow", c, c + 144, p1=1), R("pb%d" % (c // 36), 0, 144, p1=1))
         dl = "dl%d" % t
         dma("y", "so%d" % t, T[dl][me], T.srow[0:1, :], [R("srow", p1=1)], [slot(dl, me)])
         spread(lambda r: T[dl][me], T[dl][me], [slot(dl, me)], "sa%d" % t)
@@ -342,6 +351,10 @@ def rank_program(g, core, T, topo):
 
     chain = CHAIN[me]
     home = homes(chain)
+    kind = [1, 0]
+    for s in chain:
+        kind.append(1 - kind[-1] if s is None else kind[s])
+    unit = 0.125 if chain and kind[-1] == 0 else 1.0
 
     def first_list():
         cuts = (0, 320, 608, 896, 4 * C)
@@ -355,11 +368,11 @@ def rank_program(g, core, T, topo):
         tt(R("df"), nb, na, A.subtract)
         tt(R("mx"), sb, sa, A.max)
         tt(R("tt"), R("gt"), R("df"), A.mult)
-        tt(R("cc"), R("mx", 18, 36), R("mx", 0, 18), A.is_gt)
+        tt(R("cc", 18, 36), R("mx", 18, 36), R("mx", 0, 18), A.is_gt)
         tt(R("nn"), R("tt"), na, A.add)
-        tt(R("ee"), R("nn", 18, 36), R("nn", 0, 18), A.subtract)
-        tt(R("ff"), R("ee"), R("cc"), A.mult)
-        tt(R("vv"), R("ff"), R("nn", 0, 18), A.add)
+        tt(R("cc", 0, 18), R("mx", 18, 36), R("mx", 0, 18), A.is_le)
+        tt(R("ee"), R("nn"), R("cc"), A.mult)
+        tt(R("vv"), R("ee", 0, 18), R("ee", 18, 36), A.add)
         copy("v", R("ow"), R("vv"))
 
     def step(t, i, table, off, o0):
@@ -375,14 +388,23 @@ def rank_program(g, core, T, topo):
         return c0, row
 
     def wrap(i, c0, row, offsets=True):
-        y0 = C * (i % 2)
+        y0, o0 = C * (i % 2), 18 * (i % 2)
         turn(R("yy", y0, y0 + 128), R("oo", c0, c0 + 128))
         turn(R("yy", y0 + 128, y0 + C), R("oo", c0 + 128, c0 + C))
-        if offsets:
-            o0 = 18 * (i % 2)
-            copy("v", R("of", o0, o0 + 8), R("yy", y0 + row, y0 + 128, 16))
-            copy("v", R("of", o0 + 8, o0 + 18), R("yy", y0 + 128 + row, y0 + C, 16))
-        return R("yy", y0 + row, y0 + C, 16)
+        got = R("yy", y0 + row, y0 + C, 16)
+        after = (chain + [0])[i - 1] if i else None
+        if after is not None and kind[i] != after % 2:
+            ts(R("ci"), got, 0.125, A.mult)
+            ts(R("cw"), got, float(C - 16), A.mult, -float(C - 16), A.add)
+            ts(R("cx"), R("ci"), 1.0 - 8 * (C - 16), A.mult)
+            tt(R("cy"), R("cw"), R("cx"), A.add)
+            if not offsets:
+                return R("cy")
+            copy("v", R("of", o0, o0 + 18), R("cy"))
+        elif offsets:
+            ts(R("of", o0, o0 + 8), R("yy", y0 + row, y0 + 128, 16), 0.125, A.mult)
+            ts(R("of", o0 + 8, o0 + 18), R("yy", y0 + 128 + row, y0 + C, 16), 0.125, A.mult)
+        return got
 
     def unpack(t, todo, engines):
         for e in engines[:len(todo)]:
@@ -406,12 +428,13 @@ def rank_program(g, core, T, topo):
         for k, s in enumerate(chain):
             i = k + 2
             at = step(t, i, s, *(("ow", 0) if k == 0 else ("of", 18 * (k % 2 == 0))))
-            if k >= FROM[t]:
-                unpack(t, todo, "ss")
+            gap = chain[k + 1:k + 2] == [i]
+            if k >= FROM[me][t]:
+                unpack(t, todo, "sss" if gap else "ss")
             got = wrap(i, *at, offsets=k + 1 < len(chain))
-            if k >= FROM[t] and chain[k + 1:k + 2] == [k + 1] and s != k:
-                unpack(t, todo, "vvv")
-        ts(R("oz"), got, R("pf"), A.add)
+            if k >= FROM[me][t]:
+                unpack(t, todo, "vv" if me < 6 or (gap and me == 6) else "v" if gap else "")
+        ts(R("oz"), got, unit, A.mult, R("pf"), A.add)
         unpack(t, todo, "sv" * 8)
         return got
 
@@ -423,7 +446,7 @@ def rank_program(g, core, T, topo):
 
     def lists_out(got):
         name, row = PLAIN
-        copy("v", R("opl"), got)
+        ts(R("opl"), got, unit, A.mult)
         copy("s", R("pr"), R(name), R("opl"))
         for r in range(N):
             s = R("pr", 36 * r, 36 * r + 36)
@@ -434,35 +457,40 @@ def rank_program(g, core, T, topo):
 
     def take(t, k0, k1):
         zp, h = "zpb%d" % t, "hb%d" % t
+        skip = 128 - 36 if k0 == 2 else 0
         for f in (0, 1):
-            c0 = landing("b", 2 * k0 + f, t)[2]
+            c0 = landing("b", 2 * k0 + f, t)[2] - skip
             for i in range(8):
                 mm(i, *const(16 + 4 * (2 * (i // 4) + f) + i % 4), R("bq%d" % t, c0, c0 + 128), R("bs%d" % t, c0, c0 + 128),
                    f == 0, f == 1)
         for i in range(8):
             e, b = i // 4, i % 4
             for k in range(k0, k1):
-                o = 36 * (k - k0)
+                o = 36 * (k - k0) + skip
                 copy("vs"[i % 2], R(zp, C * k + 144 * e + b, C * k + 144 * e + 144, 4), R("pb%d" % i, o, o + 36))
         for k in range(k0, k1):
             for a in range(4):
                 copy("vsvv"[a], R(h, C * a, C * a + C, 1, 32 * k, 32 * k + 32), R(zp, C * k, C * k + C, 1, 32 * a, 32 * a + 32))
 
     def layer(t):
-        quant(R("hq%d" % t), R("hs%d" % t), R("hb%d" % t))
-        for b in range(4):
-            mm(b, R("wq", 128 * b, 128 * b + 128), R("wp", 128 * b, 128 * b + 128), R("hq%d" % t), R("hs%d" % t))
-        for b in range(4):
-            out, src = R("x%d" % (t + 1), b, 4 * C, 4), R("pb%d" % b, 0, C)
-            if b % 2:
-                op("s", lambda: g.scalar.activation(ap(out), ap(src), ACT.Relu, scale=0.03125), [src], [out])
-            else:
-                ts(out, src, 0.0, A.max, 0.03125, A.mult)
+        for c in (0, 144):
+            hq, hs = R("hq%d" % t, c, c + 144), R("hs%d" % t, c, c + 144)
+            quant(hq, hs, R("hb%d" % t, 4 * c, 4 * c + 576))
+            for b in range(4):
+                mm(b + c // 36, R("wq", 128 * b, 128 * b + 128), R("wp", 128 * b, 128 * b + 128), hq, hs)
+        for c in (0, 144):
+            for b in range(4):
+                out, src = R("x%d" % (t + 1), 4 * c + b, 4 * c + 576, 4), R("pb%d" % (b + c // 36), 0, 144)
+                if "vssvssvs"[b + c // 36] == "s":
+                    op("s", lambda: g.scalar.activation(ap(out), ap(src), ACT.Relu, scale=0.03125), [src], [out])
+                else:
+                    ts(out, src, 0.0, A.max, 0.03125, A.mult)
+            product(t + 1, c)
 
     dma("s", "ls", T.si[0:16, :], T.sc[:], [], [R("si", p1=16)])
     dma("y", "lx", T.x0[:], T.x[:], [], [R("x0")])
     dma("y", "lu", T.ub[:], T.u[:], [], [R("ub")])
-    iota(R("st", 0, C), [[32, 9], [C, 2], [1, 16]], 0, 0)
+    iota(R("st", 0, C), [[256, 9], [8 * C - 1, 2], [8, 16]], 1, 0)
     iota(R("tb", 0, C), [[C, 8], [1, 36]], 0, 0)
     iota(R("valm"), [[-64, 2], [0, 4], [-1, 16]], 0, 1)
     fill(R("srow", C, 384, p1=32), 0.0)
@@ -472,7 +500,7 @@ def rank_program(g, core, T, topo):
     fill(R("z", 0, HALF, p1=64), 0.0)
     parts_out(0)
     successors_out()
-    grow("st", (16, 2 * C, 4 * C))
+    grow("st", (129, 16 * C, 32 * C))
 
     for t in range(ROUNDS):
         last = t == ROUNDS - 1
@@ -492,8 +520,6 @@ def rank_program(g, core, T, topo):
         if t == 0:
             successor_offsets()
             iota(R("vale"), [[-32, 4], [256, 2], [-1, 16]], 0, 1)
-            if any(h[0] == "tc" for h in home.values()):
-                iota(R("tc"), [[0, M]], 0, 0)
         first_list()
         got = lists(t)
         serve(t)
@@ -506,10 +532,11 @@ def rank_program(g, core, T, topo):
             dma("y", "lv", T.vb[:], T.v[:], [], [R("vb")])
             dma("y", "p0", T.dp[:, 96:128, :], T.srow[0:N, C:384], [R("srow", C, 384, p1=N)], [slots("dp")])
             for u in range(ROUNDS):
-                for c in (144, SIDE + 144):
+                for c in (FILLER, SIDE + FILLER):
                     quant(R("bq%d" % u, c, c + 128), R("bs%d" % u, c, c + 128), R("x0", 0, 512))
             movers(4, "vale", [0, 256, 16, 272])
-        take(t, 0, 3)
+        take(t, 0, 2)
+        take(t, 2, 3)
         if last:
             quant(R("vq"), R("vs"), R("vb"))
             dma("y", "out", T.pl[:], T.dq[:, 0:96, :], [slots("dq")], [])
@@ -517,13 +544,12 @@ def rank_program(g, core, T, topo):
         layer(t)
 
     xq, xs = R("xq%d" % ROUNDS), R("xs%d" % ROUNDS)
-    quant(xq, xs, R("x%d" % ROUNDS))
-    mm(7, R("vq"), R("vs"), xq, xs)
     dma("y", "out", T.oc[:], bits(xq), [xq], [])
-    copy("s", R("yo"), R("pb7", 0, C))
-    dma("s", "out", T.y[:], T.yo[:], [R("yo")], [])
+    for c in (0, 144):
+        copy("v", R("yo", c, c + 144), R("pb%d" % (c // 36), 0, 144))
     for k in range(4):
-        dma("y", "out", T.osc[4 * k:4 * k + 4, :], T[xs[0]][32 * k:32 * k + 4, :], [xs], [])
+        dma("ssyy"[k], "out", T.osc[4 * k:4 * k + 4, :], T[xs[0]][32 * k:32 * k + 4, :], [xs], [])
+    dma("s", "out", T.y[:], T.yo[:], [R("yo")], [])
     for name in groups:
         wait("g", (name, None))
     for e in done:

@@ -4,13 +4,19 @@ from concourse.mybir import dt, AluOpType, ActivationFunctionType
 N, C, ROUNDS = 8, 288, 2
 M = N * C
 HALF = M // 2
-SIDE = 144 + 128
-FILLER = 112
+ODD, OWN, EVEN, LAND = C, C + 144, 2 * C + 144, 3 * C
+STRIP = 272
+FRAC = 2.0 ** -13
 Q4, U8, BF, F32, I32, U16 = "float8_e4m3fn_x4", "uint8", "bfloat16", "float32", "int32", "uint16"
 CHAIN = [[], [0, None], [None, 1, 0, 1], [0, 1, 2, 3], [0, None, 2, 3, 4, 5], [0, 1, 2, 3, 5, 6],
-         [0, 2, 3, 4, 5, 6], [0, 1, 2, 3, 5, 6, 7, 8]]
-TRADE, PLAIN = ("st", 1), ("tb", 15)
-FROM = [(2, 1)] * 6 + [(1, 1), (2, 2)]
+         [0, 1, 2, 3, 5, 6, 6, 6], [0, 1, 2, 3, 5, 6, 7, 8]]
+TRADE, PLAIN = ("st", 1), ("st", 2)
+UNPACK = [[[(0, 0)] * (2 - t) + [(2 + (CHAIN[r][k + 1:k + 2] == [k + 2]), 2) for k in range(2 - t, 8)] for r in range(6)]
+          + [[(0, 0), (0, 0), (2, 1), (2, 1), (2, 3), (2, 2), (2, 1), (2, 0)]] for t in range(ROUNDS)]
+UNPACK[0] += [[(0, 0), (0, 0), (2, 1), (2, 2), (3, 3), (2, 1), (2, 1), (2, 0)]]
+UNPACK[1] += [[(0, 0), (1, 1), (2, 1), (2, 1), (2, 3), (2, 1), (2, 1), (2, 0)]]
+MOVERS = (0, 4, 13, 16)
+HALVES = (5, 6, 7)
 
 
 def homes(chain):
@@ -29,30 +35,32 @@ def _sb(n, d):
 SCRATCH = {
     "ub": _sb(512, BF), "vb": _sb(512, BF), "uq": _sb(128, Q4), "us": _sb(128, U8), "vq": _sb(128, Q4), "vs": _sb(128, U8),
     "wq": _sb(512, Q4), "wp": _sb(512, U8),
-    "ct": _sb(8 * 516, BF), "mq": _sb(32 * 128, Q4), "ms": _sb(32 * 128, U8), "valm": _sb(128, F32), "vale": _sb(128, F32),
-    "st": _sb(M, F32), "tb": _sb(M, F32), "srow": _sb(384, F32), "sg": _sb(4 * C, F32), "sv": _sb(4 * C, F32),
+    "ct": _sb(4 * 516 + 4 * STRIP + 4, BF), "mq": _sb(2048 + 4 * STRIP, Q4), "ms": _sb(2048 + 4 * STRIP, U8),
+    "valm": _sb(128, F32), "vale": _sb(128, F32),
+    "st": _sb(M, F32), "tb": _sb(M, F32), "srow": _sb(384, F32),
     "si": _sb(72, I32), "sf": _sb(128, F32), "sx": _sb(128, F32), "rb": _sb(C, F32), "rt": _sb(C, F32), "osc16": _sb(72, U16),
-    "gt": _sb(36, F32), "mx": _sb(36, F32), "df": _sb(36, F32), "tt": _sb(36, F32), "nn": _sb(36, F32),
-    "cc": _sb(36, F32), "ee": _sb(36, F32), "vv": _sb(18, F32),
-    "ci": _sb(18, I32), "cw": _sb(18, F32), "cx": _sb(18, F32), "cy": _sb(18, F32),
+    "gt": _sb(72, F32), "mx": _sb(36, F32), "df": _sb(72, F32), "nn": _sb(72, F32),
+    "cc": _sb(36, F32), "ee": _sb(36, F32), "vv": _sb(18, F32), "ci": _sb(18, I32), "cy": _sb(18, F32),
     "oo": _sb(8 * C, F32), "yy": _sb(2 * C, F32), "of": _sb(36, U16), "ow": _sb(18, U16), "oz": _sb(18, U16), "opl": _sb(18, U16),
-    "pf": _sb(1, F32), "pr": _sb(C, F32), "yo": _sb(C, F32), "z": _sb(4 * M + HALF, BF),
+    "pf": _sb(1, F32), "bi": _sb(4, F32), "bj": _sb(4, F32), "pr": _sb(C, F32), "yo": _sb(C, F32), "z": _sb(4 * M + HALF, BF),
+    "rb1": _sb(4 * C, BF),
     "dsc": ("dram", [N, 128, 9], F32), "dp": ("dram", [N, 128, 3], F32), "dq": ("dram", [N, 128, 3], F32),
 }
+INSIDE = {"x0": ("z", 0, 4 * C), "rb0": ("z", 4 * M, 4 * C), "sg": ("tb", 0, 4 * C), "sv": ("tb", 4 * C, 4 * C)}
 for _t in range(ROUNDS + 1):
-    SCRATCH.update({"x%d" % _t: _sb(4 * C, BF), "xq%d" % _t: _sb(C, Q4), "xs%d" % _t: _sb(C, U8)})
+    SCRATCH.update({"xq%d" % _t: _sb(C, Q4), "xs%d" % _t: _sb(C, U8)})
 for _t in range(ROUNDS):
-    for _n in ("s", "g", "zp", "h"):
-        SCRATCH["%sb%d" % (_n, _t)] = _sb(4 * C, BF)
-    for _n, _w in (("s", C), ("a", C), ("g", C), ("b", 2 * SIDE + 4), ("h", C), ("ra", 72), ("rb", 72)):
+    for _n in ("sb%d" % _t, "gb%d" % _t, "zpb%d" % _t, "hb%d" % _t, "x%d" % (_t + 1)):
+        SCRATCH[_n] = _sb(4 * C, BF)
+    for _n, _w, _v in (("g", C, C), ("l", LAND, LAND), ("h", C, C), ("ra", 72, 144), ("rb", 72, 144)):
         SCRATCH["%sq%d" % (_n, _t)] = _sb(_w, Q4)
-        SCRATCH["%ss%d" % (_n, _t)] = _sb(_w, U8)
-    SCRATCH["dx%d" % _t] = ("dram", [16, N, 4 * C], BF)
+        SCRATCH["%ss%d" % (_n, _t)] = _sb(_v, U8)
+    INSIDE.update({"sq%d" % _t: ("lq%d" % _t, OWN, C), "ss%d" % _t: ("ls%d" % _t, OWN, C)})
     SCRATCH["dl%d" % _t] = ("dram", [N, 128, 3], F32)
 for _b in range(8):
     SCRATCH["pb%d" % _b] = ("psum", [128, 512], F32)
 
-_PER_ROUND = (["so", "sa", "sr", "d1_", "d2_", "ha", "raq", "ras", "rbq", "rbs", "sb"]
+_PER_ROUND = (["so", "sa", "sr", "d2_", "ha", "raq", "ras", "rbq", "rbs", "sb", "ta"]
               + ["zx%d_" % _b for _b in range(4)] + ["hb%d_" % _r for _r in range(N)] + ["bc%d_" % _l for _l in range(9)])
 SEMAPHORES = (["cv", "cs", "cp", "cg", "sent", "lx", "lu", "lv", "lw", "ls", "c0", "ca", "c1", "nu", "out", "p0", "pa"]
               + ["%s%d" % (n, t) for t in range(ROUNDS) for n in _PER_ROUND])
@@ -62,16 +70,22 @@ def relays_of(T, r, topo):
     core = T.cores[r]
     same = [c for c in topo.cores_of(core) if c != core and topo.die(c) == topo.die(core)]
     other = [c for c in topo.cores_of(core) if topo.die(c) != topo.die(core)]
-    return [(same, other)[(k + r) % 2][k // 2] for k in range(4)]
+    return [(same, other)[(k + r) % 2][k // 2] for k in range(6)]
 
 
-def served(src, k):
-    return [r for r in (2 * k, 2 * k + 1) if r != src]
+def reach(k, hop):
+    at = range(2 * k, 2 * k + 2) if k < 4 else range(4 * k - 16, 4 * k - 12)
+    return [2 * (i % 4) + i // 4 if hop == "a" else i for i in at]
+
+
+def served(src, k, hop):
+    return [r for r in reach(k, hop) if r != src]
 
 
 def landing(hop, src, t):
-    c0 = FILLER + (-72, -36, 128, -108)[src // 2] + SIDE * (src % 2) if hop == "b" else 36 * src
-    return hop + "q%d" % t, hop + "s%d" % t, c0, ("ha%d" % t if hop == "a" else "hb%d_%d" % (src, t))
+    if hop == "a":
+        return 36 * src, "ha%d" % t
+    return (ODD if src % 2 else EVEN) + 36 * (src // 2), "hb%d_%d" % (src, t)
 
 
 def transfer(topo, src, dst, engines, sem, s, d):
@@ -87,23 +101,23 @@ def share(engines, k, n):
 
 def relay_program(g, core, T, topo, src, k):
     sent = 0
-    fed = len(share(topo.engines(T.cores[src], core), k, 4))
-    to = served(src, k)
+    kind = "q" if k < 4 else "s"
     for t in range(ROUNDS):
         for hop in "ab":
-            lq, ls, c0, sem = landing(hop, src, t)
-            for kind in "qs":
-                g.wait_ge(T.sem["r%s%s%d" % (hop, kind, t)], fed)
-                ts = []
-                for i, r in enumerate(to):
-                    o = 36 * (r - 2 * k)
-                    s, d = T["r%s%s%d" % (hop, kind, t)][:, o:o + 36], T[lq if kind == "q" else ls][:, c0:c0 + 36]
-                    if kind == "q":
-                        s, d = s.bitcast(dt.uint8), d.bitcast(dt.uint8)
-                    eng = share(topo.engines(core, T.cores[r]), i, len(to))
-                    ts.append(transfer(topo, core, T.cores[r], eng, T.sem[sem], s, d))
-                    sent += len(eng)
-                g.remote_dma_fused(ts, local_sem=T.sem.sent)
+            c0, sem = landing(hop, src, t)
+            to = served(src, k, hop)
+            n = (4 if k < 4 else 2) // (2 if hop == "b" and src in HALVES else 1)
+            g.wait_ge(T.sem["r%s%s%d" % (hop, kind, t)], len(share(topo.engines(T.cores[src], core), 0, n)))
+            ts = []
+            for i, r in enumerate(to):
+                o = 36 * reach(k, hop).index(r)
+                s, d = T["r%s%s%d" % (hop, kind, t)][:, o:o + 36], T["l%s%d" % (kind, t)][:, c0:c0 + 36]
+                if kind == "q":
+                    s, d = s.bitcast(dt.uint8), d.bitcast(dt.uint8)
+                eng = share(topo.engines(core, T.cores[r]), i, len(to))
+                ts.append(transfer(topo, core, T.cores[r], eng, T.sem[sem], s, d))
+                sent += len(eng)
+            g.remote_dma_fused(ts, local_sem=T.sem.sent)
     g.wait_ge(T.sem.sent, sent)
 
 
@@ -122,6 +136,9 @@ def rank_program(g, core, T, topo):
     groups = {}
 
     def R(name, c0=0, c1=None, step=1, p0=0, p1=128):
+        if name in INSIDE:
+            name, o, w = INSIDE[name]
+            return (name, p0, p1, o + c0, o + (w if c1 is None else c1), step)
         if c1 is None:
             c1 = SCRATCH[name][1][-1]
         return (name, p0, p1, c0, c1, step)
@@ -188,6 +205,9 @@ def rank_program(g, core, T, topo):
     def bits(r):
         return ap(r).bitcast(dt.uint8)
 
+    def move(name, out, in_, view=ap, e="y"):
+        dma(e, name, view(out), view(in_), [in_], [out])
+
     others = [r for r in range(N) if r != me]
     relays = relays_of(T, me, topo)
 
@@ -240,19 +260,19 @@ def rank_program(g, core, T, topo):
         op("p", lambda: g.tensor.matmul_mx(ap(out), ap(wq), ap(ws), ap(xq), ap(xs), start, stop), [wq, ws, xq, xs], [out],
            adds=not start)
 
-    def const(k):
-        return R("mq", 128 * k, 128 * k + 128), R("ms", 128 * k, 128 * k + 128)
+    def const(c):
+        return R("mq", c, c + 128), R("ms", c, c + 128)
+
+    def shift(e, f, b):
+        return const(2048 + STRIP * b + 128 * e + 16 * (1 - f))
 
     def iota(out, pattern, base, cm):
         op("g", lambda: g.iota(ap(out), pattern, base, cm, allow_small_or_imprecise_dtypes=True), [], [out])
 
-    def plus(out, in_, c):
-        op("s", lambda: g.scalar.activation(ap(out), ap(in_), ACT.Identity, bias=c), [in_], [out])
-
-    def grow(name, first):
-        for k, c in enumerate(first):
-            w = C << k
-            plus(R(name, w, 2 * w), R(name, 0, w), float(c))
+    def grow():
+        for k in range(3):
+            out, in_, c = R("st", C << k, 2 * C << k), R("st", 0, C << k), R("bi", k, k + 1)
+            op("s", lambda: g.scalar.activation(ap(out), ap(in_), ACT.Identity, bias=ap(c)), [in_, c], [out])
 
     def slot(name, k):
         return (name, 0, 128, k, k + 1, 1)
@@ -260,42 +280,53 @@ def rank_program(g, core, T, topo):
     def slots(name):
         return (name, 0, 128, 0, N, 1)
 
-    def parts_out(t):
-        for k in range(N):
-            src = T.x[16 * k:16 * k + 16, :] if t == 0 else T["x%d" % t][16 * k:16 * k + 16, :]
-            dma("y", "d1_%d" % t, T["dx%d" % t][:, k, :], src,
-                [] if t == 0 else [R("x%d" % t, p0=16 * k, p1=16 * k + 16)], [slot("dx%d" % t, k)])
+    def runs(t):
+        who = "vvvs" if t else "vvs"
+        for i in range(32):
+            a, h, k = i // 8, i // 4 % 2, i % 4
+            c, d = 576 * h + 144 * k, 144 * (2 * a + h)
+            copy(who[i % len(who)], R("rb%d" % t, c, c + 144, 1, 32 * a, 32 * a + 32),
+                 R("x%d" % t, d, d + 144, 1, 32 * k, 32 * k + 32))
 
-    def parts_in(t):
+    def parts(t):
         for d in range(N):
-            dma("y", "d2_%d" % t, T["sb%d" % t][16 * d:16 * d + 16, :], T["dx%d" % t][:, :, 144 * d:144 * d + 144],
-                [slots("dx%d" % t)], [R("sb%d" % t, p0=16 * d, p1=16 * d + 16)])
+            for h in (0, 1):
+                p, c = 16 * (d - d % 2 + h), 576 * (d % 2)
+                move("d2_%d" % t, R("sb%d" % t, 576 * h, 576 * h + 576, 1, 16 * d, 16 * d + 16),
+                     R("rb%d" % t, c, c + 576, 1, p, p + 16), e="ys"[h * t])
 
-    def hop(src, name, t):
-        sq, ss = src + "q%d" % t, src + "s%d" % t
-        for kind, buf, view in (("q", sq, bits), ("s", ss, ap)):
-            to = "r%s%s%d" % (name, kind, t)
-            engs = [share(topo.engines(core, c), k, 4) for k, c in enumerate(relays)]
-            remote([transfer(topo, core, c, engs[k], T.sem[to], view(R(buf, 72 * k, 72 * k + 72)), view(R(to)))
-                    for k, c in enumerate(relays)], sum(len(e) for e in engs), [R(buf)],
+    def send(src, name, t, c0, c1):
+        for kind, view, first, w in (("s", ap, 4, 144), ("q", bits, 0, 72)):
+            buf, to, n = src + kind + "%d" % t, "r%s%s%d" % (name, kind, t), (c1 - c0) // w
+            via = [relays[first + c0 // w + i] for i in range(n)]
+            engs = [share(topo.engines(core, c), i, n) for i, c in enumerate(via)]
+            remote([transfer(topo, core, c, engs[i], T.sem[to], view(R(buf, c0 + w * i, c0 + w * i + w)), view(R(to)))
+                    for i, c in enumerate(via)], sum(len(e) for e in engs), [R(buf, c0, c1)],
                    "sb%d" % t if name == "b" else "sent")
-        lq, ls, c0, sem = landing(name, me, t)
-        a, b = R(sq, 36 * me, 36 * me + 36), R(ss, 36 * me, 36 * me + 36)
-        dma("y", sem, bits(R(lq, c0, c0 + 36)), bits(a), [a], [R(lq, c0, c0 + 36)])
-        dma("y", sem, ap(R(ls, c0, c0 + 36)), ap(b), [b], [R(ls, c0, c0 + 36)])
+
+    def land(src, name, t):
+        sq, ss, lq, ls = src + "q%d" % t, src + "s%d" % t, "lq%d" % t, "ls%d" % t
+        c0, sem = landing(name, me, t)
+        if name == "b":
+            wait("y", ("sb%d" % t, None))
+        o = 36 * (4 * (me % 2) + me // 2 if name == "a" else me)
+        move(sem, R(lq, c0, c0 + 36), R(sq, o, o + 36), bits)
+        move(sem, R(ls, c0, c0 + 36), R(ss, o, o + 36))
         for r in others:
-            lq, ls, c0, sem = landing(name, r, t)
-            via = relays_of(T, r, topo)[me // 2]
-            arrives(sem, 2 * len(share(topo.engines(via, core), 0, len(served(r, me // 2)))),
-                    [R(lq, c0, c0 + 36), R(ls, c0, c0 + 36)])
+            c0, sem = landing(name, r, t)
+            for k in [k for k in range(6) if me in reach(k, name)]:
+                arrives(sem, len(share(topo.engines(relays_of(T, r, topo)[k], core), 0, len(served(r, k, name)))),
+                        [R(lq if k < 4 else ls, c0, c0 + 36)])
 
     def product(t, c):
         xq, xs = R("xq%d" % t, c, c + 144), R("xs%d" % t, c, c + 144)
         quant(xq, xs, R("x%d" % t, 4 * c, 4 * c + 576))
-        if t == 0 and c == 0:
+        if t == 0 and c:
             quant(R("uq"), R("us"), R("ub"))
-        w = "v" if t == ROUNDS else "u"
-        mm(c // 36, R(w + "q"), R(w + "s"), xq, xs)
+            mm(0, R("uq"), R("us"), R("xq0", 0, 144), R("xs0", 0, 144))
+        if t or c:
+            w = "v" if t == ROUNDS else "u"
+            mm(c // 36, R(w + "q"), R(w + "s"), xq, xs)
 
     def score(t):
         if t == 0:
@@ -315,17 +346,27 @@ def rank_program(g, core, T, topo):
 
     def hop1(t):
         quant(R("sq%d" % t), R("ss%d" % t), R("sb%d" % t))
-        wait("g", ("sa%d" % t, None))
-        hop("s", "a", t)
+        if t:
+            wait("g", ("sr%d" % t, None))
+        send("s", "a", t, 0, C)
+        land("s", "a", t)
 
-    def movers(first, src, wanted):
-        fill(R("ct", 516 * first, 516 * first + 4 * 516), 0.0)
-        for i, w in enumerate(wanted):
-            d = first + i
-            ts(R("ct", 516 * d + 3, 516 * d + 515, 4), R(src), float(w), A.is_equal)
-        for k in range(4 * first, 4 * first + 16):
-            o = 516 * (k // 4) + 3 - k % 4
-            quant(*const(k), R("ct", o, o + 512))
+    def movers(part):
+        if part == 0:
+            fill(R("ct", 0, 4 * 516), 0.0)
+            for d in range(4):
+                ts(R("ct", 516 * d + 3, 516 * d + 515, 4), R("valm"), 16.0 * d, A.is_equal)
+        for j in range(MOVERS[part], MOVERS[part + 1]):
+            b, d = j // 4, j % 4
+            quant(*const(128 * j), R("ct", 516 * d + 3 - b, 516 * d + 515 - b))
+
+    def strips(part):
+        o = 4 * 516
+        for e in range(2 * (1 - part)):
+            ts(R("ct", o + 512 * e + 3, o + 512 * e + 515, 4), R("vale"), 256.0 + 16 * e, A.is_equal)
+        for b in range(4 * part):
+            c = 2048 + STRIP * b
+            quant(R("mq", c, c + STRIP), R("ms", c, c + STRIP), R("ct", o + 3 - b, o + 3 - b + 4 * STRIP))
 
     def successors_out():
         fill(R("sf", p1=32), 0.0)
@@ -338,11 +379,11 @@ def rank_program(g, core, T, topo):
         spread(lambda r: T.dsc[me], T.dsc[me], [slot("dsc", me)], "ca")
         arrives("ca", N - 1, [slot("dsc", r) for r in others])
 
-    def successors_in():
-        for r in range(N):
+    def successors_in(ranks):
+        for r in ranks:
             for k in range(4):
-                dma("ys"[k % 2], "c1", T.rb[k:128:16, 36 * r:36 * r + 36], T.dsc[r, 32 * k:32 * k + 32, :],
-                    [slots("dsc")], [R("rb", 36 * r, 36 * r + 36)])
+                dma("y" if r == me else "ys"[k % 2], "c1", T.rb[k:128:16, 36 * r:36 * r + 36], T.dsc[r, 32 * k:32 * k + 32, :],
+                    [slot("dsc", r)], [R("rb", 36 * r, 36 * r + 36)])
 
     def successor_offsets():
         turn(R("rt"), R("rb"))
@@ -354,9 +395,9 @@ def rank_program(g, core, T, topo):
     kind = [1, 0]
     for s in chain:
         kind.append(1 - kind[-1] if s is None else kind[s])
-    unit = 0.125 if chain and kind[-1] == 0 else 1.0
+    unit, zero = (1.0, 0) if not chain else (1.0, HALF) if kind[-1] == 0 else (1 / FRAC, HALF / FRAC)
 
-    def first_list():
+    def first_list(t):
         cuts = (0, 320, 608, 896, 4 * C)
         for i, e in enumerate("vsss"):
             copy(e, R("sg", cuts[i], cuts[i + 1]), R("st"), R("osc16", cuts[i] // 16, cuts[i + 1] // 16))
@@ -364,14 +405,16 @@ def rank_program(g, core, T, topo):
             turn(R("sv", cuts[i], cuts[i + 1]), R("sg", cuts[i], cuts[i + 1]))
         sa, sb = R("sv", 0, 576, 16), R("sv", 576, 1152, 16)
         na, nb = R("sv", 2, 576, 16), R("sv", 578, 1152, 16)
-        tt(R("gt"), sb, sa, A.is_gt)
-        tt(R("df"), nb, na, A.subtract)
         tt(R("mx"), sb, sa, A.max)
-        tt(R("tt"), R("gt"), R("df"), A.mult)
+        tt(R("gt", 1, 72, 2), sb, sa, A.is_gt)
+        if t == 0:
+            tt(R("df", 0, 72, 2), nb, na, A.subtract)
+            copy("v", R("df", 1, 72, 2), na)
         tt(R("cc", 18, 36), R("mx", 18, 36), R("mx", 0, 18), A.is_gt)
-        tt(R("nn"), R("tt"), na, A.add)
         tt(R("cc", 0, 18), R("mx", 18, 36), R("mx", 0, 18), A.is_le)
-        tt(R("ee"), R("nn"), R("cc"), A.mult)
+        op("v", lambda: g.vector.tensor_tensor_scan(ap(R("nn")), ap(R("gt")), ap(R("df")), 0.0, A.mult, A.add),
+           [R("gt"), R("df")], [R("nn")])
+        tt(R("ee"), R("nn", 1, 72, 2), R("cc"), A.mult)
         tt(R("vv"), R("ee", 0, 18), R("ee", 18, 36), A.add)
         copy("v", R("ow"), R("vv"))
 
@@ -383,8 +426,8 @@ def rank_program(g, core, T, topo):
         if i in home:
             to, at = home[i]
             for d in range(8):
-                dma("ys"[d % 2], "bc%d_%d" % (i, t), T[to][16 * d + at:16 * d + at + 1, :], T.oo[row:128:16, c0:c0 + C],
-                    [R("oo", c0, c0 + C)], [R(to, p0=16 * d + at, p1=16 * d + at + 1)])
+                dma("yys"[d % 3] if i == 1 else "ys"[d % 2], "bc%d_%d" % (i, t), T[to][16 * d + at:16 * d + at + 1, :],
+                    T.oo[row:128:16, c0:c0 + C], [R("oo", c0, c0 + C)], [R(to, p0=16 * d + at, p1=16 * d + at + 1)])
         return c0, row
 
     def wrap(i, c0, row, offsets=True):
@@ -394,29 +437,36 @@ def rank_program(g, core, T, topo):
         got = R("yy", y0 + row, y0 + C, 16)
         after = (chain + [0])[i - 1] if i else None
         if after is not None and kind[i] != after % 2:
-            ts(R("ci"), got, 0.125, A.mult)
-            ts(R("cw"), got, float(C - 16), A.mult, -float(C - 16), A.add)
-            ts(R("cx"), R("ci"), 1.0 - 8 * (C - 16), A.mult)
-            tt(R("cy"), R("cw"), R("cx"), A.add)
+            ts(R("ci"), got, float(HALF), A.add)
+            tt(R("cy"), got, R("ci"), A.subtract)
             if not offsets:
                 return R("cy")
-            copy("v", R("of", o0, o0 + 18), R("cy"))
+            ts(R("of", o0, o0 + 18), R("cy"), float(HALF), A.add, 1 / FRAC, A.mult)
         elif offsets:
-            ts(R("of", o0, o0 + 8), R("yy", y0 + row, y0 + 128, 16), 0.125, A.mult)
-            ts(R("of", o0 + 8, o0 + 18), R("yy", y0 + 128 + row, y0 + C, 16), 0.125, A.mult)
+            ts(R("of", o0, o0 + 8), R("yy", y0 + row, y0 + 128, 16), float(HALF), A.add)
+            ts(R("of", o0 + 8, o0 + 18), R("yy", y0 + 128 + row, y0 + C, 16), float(HALF), A.add)
         return got
 
-    def unpack(t, todo, engines):
+    ready = []
+
+    def exchange(t, most=4):
+        for b in ready[:most]:
+            own = M * b + HALF
+            for p, c in ((0, own + HALF), (64, own - HALF)):
+                move("zx%d_%d" % (b, t), R("z", c, c + HALF, 1, p, p + 64), R("z", own, own + HALF, 1, 64 - p, 128 - p))
+        del ready[:most]
+
+    def unpack(t, todo, engines, now=True):
         for e in engines[:len(todo)]:
             j = todo.pop(0)
             b, d = j // 4, j % 4
             own = M * b + HALF
-            mm(j % 7, *const(4 * d + b), R("aq%d" % t), R("as%d" % t))
+            mm(j % 7, *const(128 * j), R("lq%d" % t, 0, C), R("ls%d" % t, 0, C))
             copy(e, R("z", own + C * d, own + C * d + C), R("pb%d" % (j % 7), 0, C))
             if d == 3:
-                for p, c in ((0, own + HALF), (64, own - HALF)):
-                    o, s = R("z", c, c + HALF, 1, p, p + 64), R("z", own, own + HALF, 1, 64 - p, 128 - p)
-                    dma("y", "zx%d_%d" % (b, t), ap(o), ap(s), [s], [o])
+                ready.append(b)
+                if now:
+                    exchange(t)
 
     def lists(t):
         todo = list(range(16))
@@ -425,44 +475,59 @@ def rank_program(g, core, T, topo):
             wrap(0, *step(t, 0, None, "ow", 0))
             if 1 in home:
                 step(t, 1, None, "of", 0)
+        if t == 0:
+            movers(2)
+            strips(0)
         for k, s in enumerate(chain):
             i = k + 2
             at = step(t, i, s, *(("ow", 0) if k == 0 else ("of", 18 * (k % 2 == 0))))
-            gap = chain[k + 1:k + 2] == [i]
-            if k >= FROM[me][t]:
-                unpack(t, todo, "sss" if gap else "ss")
+            now = me < 6 or i >= max(chain)
+            exchange(t, 4 if now else 1)
+            unpack(t, todo, "s" * UNPACK[t][me][k][0], now)
             got = wrap(i, *at, offsets=k + 1 < len(chain))
-            if k >= FROM[me][t]:
-                unpack(t, todo, "vv" if me < 6 or (gap and me == 6) else "v" if gap else "")
+            unpack(t, todo, "v" * UNPACK[t][me][k][1], now)
         ts(R("oz"), got, unit, A.mult, R("pf"), A.add)
         unpack(t, todo, "sv" * 8)
+        exchange(t)
         return got
 
     def serve(t):
-        for b in range(4):
-            copy("sv"[b % 2], R("gb%d" % t, b, 4 * C, 4), R("z", M * b, M * b + M + HALF), R("oz"))
-        quant(R("gq%d" % t), R("gs%d" % t), R("gb%d" % t))
-        hop("g", "b", t)
+        def some(o0, o1, planes):
+            for b in planes:
+                copy("sv"[b % 2], R("gb%d" % t, 64 * o0 + b, 64 * o1, 4), R("z", M * b, M * b + M + HALF), R("oz", o0, o1))
+
+        def off(c0, c1):
+            quant(R("gq%d" % t, c0, c1), R("gs%d" % t, c0, c1), R("gb%d" % t, 4 * c0, 4 * c1))
+            send("g", "b", t, c0, c1)
+        if me in HALVES:
+            some(0, 10, range(4))
+            some(10, 18, range(3))
+            off(0, 144)
+            some(10, 18, [3])
+            off(144, C)
+        else:
+            some(0, 18, range(4))
+            off(0, C)
+        land("g", "b", t)
 
     def lists_out(got):
         name, row = PLAIN
-        ts(R("opl"), got, unit, A.mult)
+        ts(R("opl"), got, unit, A.mult, float(zero), A.add)
         copy("s", R("pr"), R(name), R("opl"))
         for r in range(N):
             s = R("pr", 36 * r, 36 * r + 36)
             to, sem = ("dq", "pa") if r == me else ("dp", "p0")
-            dma("s", sem, T[to][r, 0:96, :], T.pr[row:128:16, 36 * r:36 * r + 36], [s], [slot(to, r)])
+            dma("y", sem, T[to][r, 0:96, :], T.pr[row:128:16, 36 * r:36 * r + 36], [s], [slot(to, r)])
         spread(lambda r: T.dp[r], T.dq[me], [slots("dp")], "pa")
         arrives("pa", N - 1, [slot("dq", r) for r in others])
 
     def take(t, k0, k1):
         zp, h = "zpb%d" % t, "hb%d" % t
-        skip = 128 - 36 if k0 == 2 else 0
+        skip = 128 - 36 * (k1 - k0)
         for f in (0, 1):
-            c0 = landing("b", 2 * k0 + f, t)[2] - skip
+            c0 = landing("b", 2 * k0 + f, t)[0] - skip
             for i in range(8):
-                mm(i, *const(16 + 4 * (2 * (i // 4) + f) + i % 4), R("bq%d" % t, c0, c0 + 128), R("bs%d" % t, c0, c0 + 128),
-                   f == 0, f == 1)
+                mm(i, *shift(i // 4, f, i % 4), R("lq%d" % t, c0, c0 + 128), R("ls%d" % t, c0, c0 + 128), f == 0, f == 1)
         for i in range(8):
             e, b = i // 4, i % 4
             for k in range(k0, k1):
@@ -470,7 +535,11 @@ def rank_program(g, core, T, topo):
                 copy("vs"[i % 2], R(zp, C * k + 144 * e + b, C * k + 144 * e + 144, 4), R("pb%d" % i, o, o + 36))
         for k in range(k0, k1):
             for a in range(4):
-                copy("vsvv"[a], R(h, C * a, C * a + C, 1, 32 * k, 32 * k + 32), R(zp, C * k, C * k + C, 1, 32 * a, 32 * a + 32))
+                o, s = R(h, C * a, C * a + C, 1, 32 * k, 32 * k + 32), R(zp, C * k, C * k + C, 1, 32 * a, 32 * a + 32)
+                if k < 2:
+                    move("ta%d" % t, o, s)
+                else:
+                    copy("vvsv"[a], o, s)
 
     def layer(t):
         for c in (0, 144):
@@ -481,75 +550,82 @@ def rank_program(g, core, T, topo):
         for c in (0, 144):
             for b in range(4):
                 out, src = R("x%d" % (t + 1), 4 * c + b, 4 * c + 576, 4), R("pb%d" % (b + c // 36), 0, 144)
-                if "vssvssvs"[b + c // 36] == "s":
+                if b % 2 == 0:
                     op("s", lambda: g.scalar.activation(ap(out), ap(src), ACT.Relu, scale=0.03125), [src], [out])
                 else:
                     ts(out, src, 0.0, A.max, 0.03125, A.mult)
             product(t + 1, c)
 
     dma("s", "ls", T.si[0:16, :], T.sc[:], [], [R("si", p1=16)])
-    dma("y", "lx", T.x0[:], T.x[:], [], [R("x0")])
-    dma("y", "lu", T.ub[:], T.u[:], [], [R("ub")])
-    iota(R("st", 0, C), [[256, 9], [8 * C - 1, 2], [8, 16]], 1, 0)
-    iota(R("tb", 0, C), [[C, 8], [1, 36]], 0, 0)
+    dma("y", "lx", ap(R("x0")), T.x[:], [], [R("x0")])
+    iota(R("sg", 0, C), [[32, 9], [C, 2], [1, 16]], -HALF, 0)
+    iota(R("sv", 0, C), [[1, C]], 0, 0)
+    iota(R("rt"), [[C, 8], [1, 36]], 0, 0)
     iota(R("valm"), [[-64, 2], [0, 4], [-1, 16]], 0, 1)
+    for k in range(4):
+        fill(R("bi", k, k + 1), (16 + C * FRAC, 2 * C * (1 + FRAC), 4 * C * (1 + FRAC), 0.0)[k])
+        fill(R("bj", k, k + 1), 36.0 * 2 ** k)
     fill(R("srow", C, 384, p1=32), 0.0)
-    fill(R("rb"), 0.0)
-    fill(R("pf", p1=64), float(HALF))
-    fill(R("pf", p0=64), 0.0)
-    fill(R("z", 0, HALF, p1=64), 0.0)
-    parts_out(0)
     successors_out()
-    grow("st", (129, 16 * C, 32 * C))
+    fill(R("rb"), 0.0)
+    dma("y", "lu", T.ub[:], T.u[:], [], [R("ub")])
+    ts(R("sv", C, 2 * C), R("sv", 0, C), FRAC, A.mult)
+    tt(R("st", 0, C), R("sg", 0, C), R("sv", C, 2 * C), A.add)
+    dma("y", "nu", T.st[2:128:16, 0:C], T.rt[2:128:16, :], [R("rt")], [R("st", 0, C)])
+    dma("y", "nu", T.bi[2:128:16, :], T.bj[2:128:16, :], [R("bj")], [R("bi")])
+    dma("y", "lw", bits(R("wq")), T.wc[:], [], [R("wq")])
+    dma("y", "lw", T.wp[:], T.ws[:], [], [R("wp")])
 
     for t in range(ROUNDS):
         last = t == ROUNDS - 1
-        if t:
-            parts_out(t)
-        score(t)
         if t == 0:
-            grow("tb", (36, 72, 144))
-            dma("s", "nu", T.st[2:128:16, :], T.tb[2:128:16, :], [R("tb")], [R("st")])
-            movers(0, "valm", [0, 16, 32, 48])
-            fill(R("z", 4 * M, 4 * M + HALF, p0=64), 0.0)
-        parts_in(t)
-        if t == 0:
-            successors_in()
+            runs(t)
+            parts(t)
+            score(t)
+            fill(R("gt"), 0.0)
+            successors_in([me])
+            grow()
+            movers(0)
+            successors_in(others)
+        else:
+            score(t)
+            runs(t)
+            quant(R("vq"), R("vs"), R("vb"))
+            parts(t)
         score_rows(t)
         hop1(t)
         if t == 0:
-            successor_offsets()
+            movers(1)
             iota(R("vale"), [[-32, 4], [256, 2], [-1, 16]], 0, 1)
-        first_list()
+            fill(R("ct", 4 * 516), 0.0)
+            fill(R("pf", p1=64), float(HALF + zero))
+            fill(R("pf", p0=64), float(zero))
+            successor_offsets()
+            dma("y", "p0", T.dp[:, 96:128, :], T.srow[0:N, C:384], [R("srow", C, 384, p1=N)], [slots("dp")])
+        first_list(t)
         got = lists(t)
         serve(t)
         if last:
             lists_out(got)
-        if t == 0:
-            wait("y", ("sb0", None))
-            dma("y", "lw", bits(R("wq")), T.wc[:], [], [R("wq")])
-            dma("y", "lw", T.wp[:], T.ws[:], [], [R("wp")])
+        else:
             dma("y", "lv", T.vb[:], T.v[:], [], [R("vb")])
-            dma("y", "p0", T.dp[:, 96:128, :], T.srow[0:N, C:384], [R("srow", C, 384, p1=N)], [slots("dp")])
-            for u in range(ROUNDS):
-                for c in (FILLER, SIDE + FILLER):
-                    quant(R("bq%d" % u, c, c + 128), R("bs%d" % u, c, c + 128), R("x0", 0, 512))
-            movers(4, "vale", [0, 256, 16, 272])
+            strips(1)
         take(t, 0, 2)
         take(t, 2, 3)
         if last:
-            quant(R("vq"), R("vs"), R("vb"))
             dma("y", "out", T.pl[:], T.dq[:, 0:96, :], [slots("dq")], [])
         take(t, 3, 4)
         layer(t)
 
     xq, xs = R("xq%d" % ROUNDS), R("xs%d" % ROUNDS)
-    dma("y", "out", T.oc[:], bits(xq), [xq], [])
     for c in (0, 144):
-        copy("v", R("yo", c, c + 144), R("pb%d" % (c // 36), 0, 144))
-    for k in range(4):
-        dma("ssyy"[k], "out", T.osc[4 * k:4 * k + 4, :], T[xs[0]][32 * k:32 * k + 4, :], [xs], [])
-    dma("s", "out", T.y[:], T.yo[:], [R("yo")], [])
+        half = R(xq[0], c, c + 144)
+        dma("y", "out", T.oc[:, 4 * c:4 * c + 576], bits(half), [half], [])
+        if c:
+            for k in range(4):
+                dma("yyss"[k], "out", T.osc[4 * k:4 * k + 4, :], T[xs[0]][32 * k:32 * k + 4, :], [xs], [])
+        copy("sv"[c // 144], R("yo", c, c + 144), R("pb%d" % (c // 36), 0, 144))
+        dma("ys"[c // 144], "out", T.y[:, c:c + 144], T.yo[:, c:c + 144], [R("yo", c, c + 144)], [])
     for name in groups:
         wait("g", (name, None))
     for e in done:

from concourse.bass import DstId, RemoteDMATransfer
from concourse.mybir import dt, AluOpType, ActivationFunctionType

N, C, ROUNDS = 8, 288, 2
M = N * C
HALF = M // 2
ODD, OWN, EVEN, LAND = C, C + 144, 2 * C + 144, 3 * C
STRIP = 272
FRAC = 2.0 ** -13
Q4, U8, BF, F32, I32, U16 = "float8_e4m3fn_x4", "uint8", "bfloat16", "float32", "int32", "uint16"
CHAIN = [[], [0, None], [None, 1, 0, 1], [0, 1, 2, 3], [0, None, 2, 3, 4, 5], [0, 1, 2, 3, 5, 6],
         [0, 1, 2, 3, 5, 6, 6, 6], [0, 1, 2, 3, 5, 6, 7, 8]]
TRADE, PLAIN = ("st", 1), ("st", 2)
UNPACK = [[[(0, 0)] * (2 - t) + [(2 + (CHAIN[r][k + 1:k + 2] == [k + 2]), 2) for k in range(2 - t, 8)] for r in range(6)]
          + [[(0, 0), (0, 0), (2, 1), (2, 1), (2, 3), (2, 2), (2, 1), (2, 0)]] for t in range(ROUNDS)]
UNPACK[0] += [[(0, 0), (0, 0), (2, 1), (2, 2), (3, 3), (2, 1), (2, 1), (2, 0)]]
UNPACK[1] += [[(0, 0), (1, 1), (2, 1), (2, 1), (2, 3), (2, 1), (2, 1), (2, 0)]]
MOVERS = (0, 4, 13, 16)
HALVES = (5, 6, 7)


def homes(chain):
    at = {None: TRADE}
    reads = [None] + list(chain)
    for s in sorted(set(chain) - {None}):
        busy = {at[u][0] for u in reads[s:s + 2] if u in at}
        at[s] = ([b for b in ("st", "tb") if b not in busy][0], 3 + s)
    return at


def _sb(n, d):
    return ("sbuf", [128, n], d)


SCRATCH = {
    "ub": _sb(512, BF), "vb": _sb(512, BF), "uq": _sb(128, Q4), "us": _sb(128, U8), "vq": _sb(128, Q4), "vs": _sb(128, U8),
    "wq": _sb(512, Q4), "wp": _sb(512, U8),
    "ct": _sb(4 * 516 + 4 * STRIP + 4, BF), "mq": _sb(2048 + 4 * STRIP, Q4), "ms": _sb(2048 + 4 * STRIP, U8),
    "valm": _sb(128, F32), "vale": _sb(128, F32),
    "st": _sb(M, F32), "tb": _sb(M, F32), "srow": _sb(384, F32),
    "si": _sb(72, I32), "sf": _sb(128, F32), "sx": _sb(128, F32), "rb": _sb(C, F32), "rt": _sb(C, F32), "osc16": _sb(72, U16),
    "gt": _sb(72, F32), "mx": _sb(36, F32), "df": _sb(72, F32), "nn": _sb(72, F32),
    "cc": _sb(36, F32), "ee": _sb(36, F32), "vv": _sb(18, F32), "ci": _sb(18, I32), "cy": _sb(18, F32),
    "oo": _sb(8 * C, F32), "yy": _sb(2 * C, F32), "of": _sb(36, U16), "ow": _sb(18, U16), "oz": _sb(18, U16), "opl": _sb(18, U16),
    "pf": _sb(1, F32), "bi": _sb(4, F32), "bj": _sb(4, F32), "pr": _sb(C, F32), "yo": _sb(C, F32), "z": _sb(4 * M + HALF, BF),
    "rb1": _sb(4 * C, BF),
    "dsc": ("dram", [N, 128, 9], F32), "dp": ("dram", [N, 128, 3], F32), "dq": ("dram", [N, 128, 3], F32),
}
INSIDE = {"x0": ("z", 0, 4 * C), "rb0": ("z", 4 * M, 4 * C), "sg": ("tb", 0, 4 * C), "sv": ("tb", 4 * C, 4 * C)}
for _t in range(ROUNDS + 1):
    SCRATCH.update({"xq%d" % _t: _sb(C, Q4), "xs%d" % _t: _sb(C, U8)})
for _t in range(ROUNDS):
    for _n in ("sb%d" % _t, "gb%d" % _t, "zpb%d" % _t, "hb%d" % _t, "x%d" % (_t + 1)):
        SCRATCH[_n] = _sb(4 * C, BF)
    for _n, _w, _v in (("g", C, C), ("l", LAND, LAND), ("h", C, C), ("ra", 72, 144), ("rb", 72, 144)):
        SCRATCH["%sq%d" % (_n, _t)] = _sb(_w, Q4)
        SCRATCH["%ss%d" % (_n, _t)] = _sb(_v, U8)
    INSIDE.update({"sq%d" % _t: ("lq%d" % _t, OWN, C), "ss%d" % _t: ("ls%d" % _t, OWN, C)})
    SCRATCH["dl%d" % _t] = ("dram", [N, 128, 3], F32)
for _b in range(8):
    SCRATCH["pb%d" % _b] = ("psum", [128, 512], F32)

_PER_ROUND = (["so", "sa", "sr", "d2_", "ha", "raq", "ras", "rbq", "rbs", "sb", "ta"]
              + ["zx%d_" % _b for _b in range(4)] + ["hb%d_" % _r for _r in range(N)] + ["bc%d_" % _l for _l in range(9)])
SEMAPHORES = (["cv", "cs", "cp", "cg", "sent", "lx", "lu", "lv", "lw", "ls", "c0", "ca", "c1", "nu", "out", "p0", "pa"]
              + ["%s%d" % (n, t) for t in range(ROUNDS) for n in _PER_ROUND])


def relays_of(T, r, topo):
    core = T.cores[r]
    same = [c for c in topo.cores_of(core) if c != core and topo.die(c) == topo.die(core)]
    other = [c for c in topo.cores_of(core) if topo.die(c) != topo.die(core)]
    return [(same, other)[(k + r) % 2][k // 2] for k in range(6)]


def reach(k, hop):
    at = range(2 * k, 2 * k + 2) if k < 4 else range(4 * k - 16, 4 * k - 12)
    return [2 * (i % 4) + i // 4 if hop == "a" else i for i in at]


def served(src, k, hop):
    return [r for r in reach(k, hop) if r != src]


def landing(hop, src, t):
    if hop == "a":
        return 36 * src, "ha%d" % t
    return (ODD if src % 2 else EVEN) + 36 * (src // 2), "hb%d_%d" % (src, t)


def transfer(topo, src, dst, engines, sem, s, d):
    rid, pid = topo.addr(dst, src)
    return RemoteDMATransfer(dst_ids=[DstId(rid=rid, pnc=pid)], dma_engine_mask=sum(1 << e for e in engines),
                             remote_sem=sem, src=s, dst=d)


def share(engines, k, n):
    w = len(engines) // n
    return engines[w * k:w * k + w]


def relay_program(g, core, T, topo, src, k):
    sent = 0
    kind = "q" if k < 4 else "s"
    for t in range(ROUNDS):
        for hop in "ab":
            c0, sem = landing(hop, src, t)
            to = served(src, k, hop)
            n = (4 if k < 4 else 2) // (2 if hop == "b" and src in HALVES else 1)
            g.wait_ge(T.sem["r%s%s%d" % (hop, kind, t)], len(share(topo.engines(T.cores[src], core), 0, n)))
            ts = []
            for i, r in enumerate(to):
                o = 36 * reach(k, hop).index(r)
                s, d = T["r%s%s%d" % (hop, kind, t)][:, o:o + 36], T["l%s%d" % (kind, t)][:, c0:c0 + 36]
                if kind == "q":
                    s, d = s.bitcast(dt.uint8), d.bitcast(dt.uint8)
                eng = share(topo.engines(core, T.cores[r]), i, len(to))
                ts.append(transfer(topo, core, T.cores[r], eng, T.sem[sem], s, d))
                sent += len(eng)
            g.remote_dma_fused(ts, local_sem=T.sem.sent)
    g.wait_ge(T.sem.sent, sent)


def rank_program(g, core, T, topo):
    me = T.rank_of(core)
    if me is None:
        for r in range(N):
            if core in relays_of(T, r, topo):
                relay_program(g, core, T, topo, r, relays_of(T, r, topo).index(core))
        return
    A, ACT = AluOpType, ActivationFunctionType
    queue = {"v": g.vector, "s": g.scalar, "p": g.tensor, "g": g, "y": g.sync}
    done = {e: {"sem": "c" + e, "n": 0} for e in "vspg"}
    waited = {e: {} for e in queue}
    log = {}
    groups = {}

    def R(name, c0=0, c1=None, step=1, p0=0, p1=128):
        if name in INSIDE:
            name, o, w = INSIDE[name]
            return (name, p0, p1, o + c0, o + (w if c1 is None else c1), step)
        if c1 is None:
            c1 = SCRATCH[name][1][-1]
        return (name, p0, p1, c0, c1, step)

    def ap(r):
        return T[r[0]][r[1]:r[2], r[3]:r[4]:r[5]] if r[5] > 1 else T[r[0]][r[1]:r[2], r[3]:r[4]]

    def meet(a, b):
        if a[2] <= b[1] or b[2] <= a[1] or a[4] <= b[3] or b[4] <= a[3]:
            return False
        if a[5] == b[5]:
            return (a[3] - b[3]) % a[5] == 0
        return bool(set(range(a[3], a[4], a[5])) & set(range(b[3], b[4], b[5])))

    def wait(e, tok):
        if tok[1] is None:
            grp = groups[tok[0]]
            grp["shut"] = True
            n = grp["n"]
        else:
            n = tok[1]
        if waited[e].get(tok[0], 0) < n:
            queue[e].wait_ge(T.sem[tok[0]], n)
            waited[e][tok[0]] = n

    def order(e, reads, writes, own=None, adds=False):
        need = {}
        for r, w in [(r, False) for r in reads] + [(r, True) for r in writes]:
            bank = r[0].startswith("pb")
            if bank and adds:
                continue
            for (o, ow, tok, oe) in log.get(r[0], []):
                if tok[0] == own:
                    continue
                if (bank and (oe != e or w or ow)) or (not bank and (w or ow) and meet(r, o)):
                    if tok[1] is None or need.get(tok[0], 0) < tok[1]:
                        need[tok[0]] = tok[1]
        for s in need:
            wait(e, (s, need[s]))

    def note(e, tok, reads, writes):
        for r in reads:
            log.setdefault(r[0], []).append((r, False, tok, e))
        for r in writes:
            log.setdefault(r[0], []).append((r, True, tok, e))

    def op(e, call, reads, writes, adds=False):
        order(e, reads, writes, adds=adds)
        done[e]["n"] += 1
        call().then_inc(T.sem[done[e]["sem"]], 1)
        note(e, (done[e]["sem"], done[e]["n"]), reads, writes)

    def more(name, n):
        grp = groups.setdefault(name, {"n": 0, "shut": False})
        assert not grp["shut"], name
        grp["n"] += n

    def dma(e, name, out, in_, reads, writes):
        order(e, reads, writes, own=name)
        more(name, 16)
        queue[e].dma_start(out, in_).then_inc(T.sem[name], 16)
        note(e, (name, None), reads, writes)

    def bits(r):
        return ap(r).bitcast(dt.uint8)

    def move(name, out, in_, view=ap, e="y"):
        dma(e, name, view(out), view(in_), [in_], [out])

    others = [r for r in range(N) if r != me]
    relays = relays_of(T, me, topo)

    def remote(ts, n, reads, left="sent"):
        order("g", reads, [], own=left)
        g.remote_dma_fused(ts, local_sem=T.sem[left])
        more(left, n)
        note("g", (left, None), reads, [])

    def spread(piece, to, reads, sem):
        remote([transfer(topo, core, T.cores[r], [topo.engines(core, T.cores[r])[i]], T.sem[sem], piece(r), to)
                for i, r in enumerate(others)], len(others), reads)

    def arrives(sem, n, writes):
        more(sem, n)
        note("g", (sem, None), [], writes)

    def val(x):
        return ap(x) if isinstance(x, tuple) else x

    def copy(e, out, in_, offs=None):
        src = ap(in_) if offs is None else ap(in_).indirect(ap(offs))
        rd = [in_] if offs is None else [in_, offs]
        if e == "v":
            op(e, lambda: g.vector.tensor_copy(ap(out), src), rd, [out])
        else:
            op(e, lambda: g.scalar.activation(ap(out), src, ACT.Copy), rd, [out])

    def tt(out, a, b, alu):
        op("v", lambda: g.vector.tensor_tensor(ap(out), ap(a), ap(b), alu), [a, b], [out])

    def ts(out, a, s1, o1, s2=None, o2=None):
        rd = [a] + [s for s in (s1, s2) if isinstance(s, tuple)]
        if s2 is None:
            op("v", lambda: g.vector.tensor_scalar(ap(out), ap(a), val(s1), None, o1), rd, [out])
        else:
            op("v", lambda: g.vector.tensor_scalar(ap(out), ap(a), val(s1), val(s2), o1, o2), rd, [out])

    def fill(out, c):
        op("v", lambda: g.vector.memset(ap(out), c), [], [out])

    def turn(out, in_):
        op("v", lambda: g.vector.transpose(ap(out), ap(in_)), [in_], [out])

    def quant(q, s, in_):
        op("v", lambda: g.vector.quantize_mx(ap(q), ap(s), ap(in_)), [in_], [q, s])

    def mm(bank, wq, ws, xq, xs, start=True, stop=True):
        out = R("pb%d" % bank, 0, xq[4] - xq[3])
        op("p", lambda: g.tensor.matmul_mx(ap(out), ap(wq), ap(ws), ap(xq), ap(xs), start, stop), [wq, ws, xq, xs], [out],
           adds=not start)

    def const(c):
        return R("mq", c, c + 128), R("ms", c, c + 128)

    def shift(e, f, b):
        return const(2048 + STRIP * b + 128 * e + 16 * (1 - f))

    def iota(out, pattern, base, cm):
        op("g", lambda: g.iota(ap(out), pattern, base, cm, allow_small_or_imprecise_dtypes=True), [], [out])

    def grow():
        for k in range(3):
            out, in_, c = R("st", C << k, 2 * C << k), R("st", 0, C << k), R("bi", k, k + 1)
            op("s", lambda: g.scalar.activation(ap(out), ap(in_), ACT.Identity, bias=ap(c)), [in_, c], [out])

    def slot(name, k):
        return (name, 0, 128, k, k + 1, 1)

    def slots(name):
        return (name, 0, 128, 0, N, 1)

    def runs(t):
        who = "vvvs" if t else "vvs"
        for i in range(32):
            a, h, k = i // 8, i // 4 % 2, i % 4
            c, d = 576 * h + 144 * k, 144 * (2 * a + h)
            copy(who[i % len(who)], R("rb%d" % t, c, c + 144, 1, 32 * a, 32 * a + 32),
                 R("x%d" % t, d, d + 144, 1, 32 * k, 32 * k + 32))

    def parts(t):
        for d in range(N):
            for h in (0, 1):
                p, c = 16 * (d - d % 2 + h), 576 * (d % 2)
                move("d2_%d" % t, R("sb%d" % t, 576 * h, 576 * h + 576, 1, 16 * d, 16 * d + 16),
                     R("rb%d" % t, c, c + 576, 1, p, p + 16), e="ys"[h * t])

    def send(src, name, t, c0, c1):
        for kind, view, first, w in (("s", ap, 4, 144), ("q", bits, 0, 72)):
            buf, to, n = src + kind + "%d" % t, "r%s%s%d" % (name, kind, t), (c1 - c0) // w
            via = [relays[first + c0 // w + i] for i in range(n)]
            engs = [share(topo.engines(core, c), i, n) for i, c in enumerate(via)]
            remote([transfer(topo, core, c, engs[i], T.sem[to], view(R(buf, c0 + w * i, c0 + w * i + w)), view(R(to)))
                    for i, c in enumerate(via)], sum(len(e) for e in engs), [R(buf, c0, c1)],
                   "sb%d" % t if name == "b" else "sent")

    def land(src, name, t):
        sq, ss, lq, ls = src + "q%d" % t, src + "s%d" % t, "lq%d" % t, "ls%d" % t
        c0, sem = landing(name, me, t)
        if name == "b":
            wait("y", ("sb%d" % t, None))
        o = 36 * (4 * (me % 2) + me // 2 if name == "a" else me)
        move(sem, R(lq, c0, c0 + 36), R(sq, o, o + 36), bits)
        move(sem, R(ls, c0, c0 + 36), R(ss, o, o + 36))
        for r in others:
            c0, sem = landing(name, r, t)
            for k in [k for k in range(6) if me in reach(k, name)]:
                arrives(sem, len(share(topo.engines(relays_of(T, r, topo)[k], core), 0, len(served(r, k, name)))),
                        [R(lq if k < 4 else ls, c0, c0 + 36)])

    def product(t, c):
        xq, xs = R("xq%d" % t, c, c + 144), R("xs%d" % t, c, c + 144)
        quant(xq, xs, R("x%d" % t, 4 * c, 4 * c + 576))
        if t == 0 and c:
            quant(R("uq"), R("us"), R("ub"))
            mm(0, R("uq"), R("us"), R("xq0", 0, 144), R("xs0", 0, 144))
        if t or c:
            w = "v" if t == ROUNDS else "u"
            mm(c // 36, R(w + "q"), R(w + "s"), xq, xs)

    def score(t):
        if t == 0:
            product(0, 0)
            product(0, 144)
        for c in (0, 144):
            copy("s" if t and not c else "v", R("srow", c, c + 144, p1=1), R("pb%d" % (c // 36), 0, 144, p1=1))
        dl = "dl%d" % t
        dma("y", "so%d" % t, T[dl][me], T.srow[0:1, :], [R("srow", p1=1)], [slot(dl, me)])
        spread(lambda r: T[dl][me], T[dl][me], [slot(dl, me)], "sa%d" % t)
        arrives("sa%d" % t, N - 1, [slot(dl, r) for r in others])

    def score_rows(t):
        for k in range(8):
            dma("ys"[k % 2], "sr%d" % t, T.st[16 * k:16 * k + 1, :], T["dl%d" % t][:, 0:96, :],
                [slots("dl%d" % t)], [R("st", p0=16 * k, p1=16 * k + 1)])

    def hop1(t):
        quant(R("sq%d" % t), R("ss%d" % t), R("sb%d" % t))
        if t:
            wait("g", ("sr%d" % t, None))
        send("s", "a", t, 0, C)
        land("s", "a", t)

    def movers(part):
        if part == 0:
            fill(R("ct", 0, 4 * 516), 0.0)
            for d in range(4):
                ts(R("ct", 516 * d + 3, 516 * d + 515, 4), R("valm"), 16.0 * d, A.is_equal)
        for j in range(MOVERS[part], MOVERS[part + 1]):
            b, d = j // 4, j % 4
            quant(*const(128 * j), R("ct", 516 * d + 3 - b, 516 * d + 515 - b))

    def strips(part):
        o = 4 * 516
        for e in range(2 * (1 - part)):
            ts(R("ct", o + 512 * e + 3, o + 512 * e + 515, 4), R("vale"), 256.0 + 16 * e, A.is_equal)
        for b in range(4 * part):
            c = 2048 + STRIP * b
            quant(R("mq", c, c + STRIP), R("ms", c, c + STRIP), R("ct", o + 3 - b, o + 3 - b + 4 * STRIP))

    def successors_out():
        fill(R("sf", p1=32), 0.0)
        for k in range(4):
            copy("v", R("sf", 32 * k, 32 * k + 18, p1=16), R("si", 18 * k, 18 * k + 18, p1=16))
        turn(R("sx", p1=32), R("sf", p1=32))
        for k in range(4):
            s = R("sx", 32 * k, 32 * k + 16, p1=18)
            dma("ys"[k % 2], "c0", T.dsc[me, 32 * k:32 * k + 32, :], ap(s), [s], [slot("dsc", me)])
        spread(lambda r: T.dsc[me], T.dsc[me], [slot("dsc", me)], "ca")
        arrives("ca", N - 1, [slot("dsc", r) for r in others])

    def successors_in(ranks):
        for r in ranks:
            for k in range(4):
                dma("y" if r == me else "ys"[k % 2], "c1", T.rb[k:128:16, 36 * r:36 * r + 36], T.dsc[r, 32 * k:32 * k + 32, :],
                    [slot("dsc", r)], [R("rb", 36 * r, 36 * r + 36)])

    def successor_offsets():
        turn(R("rt"), R("rb"))
        for k, kk in enumerate((0, 2, 1, 3)):
            copy("v", R("osc16", 18 * k, 18 * k + 18), R("rt", kk, C, 16))

    chain = CHAIN[me]
    home = homes(chain)
    kind = [1, 0]
    for s in chain:
        kind.append(1 - kind[-1] if s is None else kind[s])
    unit, zero = (1.0, 0) if not chain else (1.0, HALF) if kind[-1] == 0 else (1 / FRAC, HALF / FRAC)

    def first_list(t):
        cuts = (0, 320, 608, 896, 4 * C)
        for i, e in enumerate("vsss"):
            copy(e, R("sg", cuts[i], cuts[i + 1]), R("st"), R("osc16", cuts[i] // 16, cuts[i + 1] // 16))
        for i in range(4):
            turn(R("sv", cuts[i], cuts[i + 1]), R("sg", cuts[i], cuts[i + 1]))
        sa, sb = R("sv", 0, 576, 16), R("sv", 576, 1152, 16)
        na, nb = R("sv", 2, 576, 16), R("sv", 578, 1152, 16)
        tt(R("mx"), sb, sa, A.max)
        tt(R("gt", 1, 72, 2), sb, sa, A.is_gt)
        if t == 0:
            tt(R("df", 0, 72, 2), nb, na, A.subtract)
            copy("v", R("df", 1, 72, 2), na)
        tt(R("cc", 18, 36), R("mx", 18, 36), R("mx", 0, 18), A.is_gt)
        tt(R("cc", 0, 18), R("mx", 18, 36), R("mx", 0, 18), A.is_le)
        op("v", lambda: g.vector.tensor_tensor_scan(ap(R("nn")), ap(R("gt")), ap(R("df")), 0.0, A.mult, A.add),
           [R("gt"), R("df")], [R("nn")])
        tt(R("ee"), R("nn", 1, 72, 2), R("cc"), A.mult)
        tt(R("vv"), R("ee", 0, 18), R("ee", 18, 36), A.add)
        copy("v", R("ow"), R("vv"))

    def step(t, i, table, off, o0):
        name, row = home[table]
        c0 = C * (i % 8)
        copy("v", R("oo", c0, c0 + 128), R(name), R(off, o0, o0 + 8))
        copy("s", R("oo", c0 + 128, c0 + C), R(name), R(off, o0 + 8, o0 + 18))
        if i in home:
            to, at = home[i]
            for d in range(8):
                dma("yys"[d % 3] if i == 1 else "ys"[d % 2], "bc%d_%d" % (i, t), T[to][16 * d + at:16 * d + at + 1, :],
                    T.oo[row:128:16, c0:c0 + C], [R("oo", c0, c0 + C)], [R(to, p0=16 * d + at, p1=16 * d + at + 1)])
        return c0, row

    def wrap(i, c0, row, offsets=True):
        y0, o0 = C * (i % 2), 18 * (i % 2)
        turn(R("yy", y0, y0 + 128), R("oo", c0, c0 + 128))
        turn(R("yy", y0 + 128, y0 + C), R("oo", c0 + 128, c0 + C))
        got = R("yy", y0 + row, y0 + C, 16)
        after = (chain + [0])[i - 1] if i else None
        if after is not None and kind[i] != after % 2:
            ts(R("ci"), got, float(HALF), A.add)
            tt(R("cy"), got, R("ci"), A.subtract)
            if not offsets:
                return R("cy")
            ts(R("of", o0, o0 + 18), R("cy"), float(HALF), A.add, 1 / FRAC, A.mult)
        elif offsets:
            ts(R("of", o0, o0 + 8), R("yy", y0 + row, y0 + 128, 16), float(HALF), A.add)
            ts(R("of", o0 + 8, o0 + 18), R("yy", y0 + 128 + row, y0 + C, 16), float(HALF), A.add)
        return got

    ready = []

    def exchange(t, most=4):
        for b in ready[:most]:
            own = M * b + HALF
            for p, c in ((0, own + HALF), (64, own - HALF)):
                move("zx%d_%d" % (b, t), R("z", c, c + HALF, 1, p, p + 64), R("z", own, own + HALF, 1, 64 - p, 128 - p))
        del ready[:most]

    def unpack(t, todo, engines, now=True):
        for e in engines[:len(todo)]:
            j = todo.pop(0)
            b, d = j // 4, j % 4
            own = M * b + HALF
            mm(j % 7, *const(128 * j), R("lq%d" % t, 0, C), R("ls%d" % t, 0, C))
            copy(e, R("z", own + C * d, own + C * d + C), R("pb%d" % (j % 7), 0, C))
            if d == 3:
                ready.append(b)
                if now:
                    exchange(t)

    def lists(t):
        todo = list(range(16))
        got = R("vv")
        if chain:
            wrap(0, *step(t, 0, None, "ow", 0))
            if 1 in home:
                step(t, 1, None, "of", 0)
        if t == 0:
            movers(2)
            strips(0)
        for k, s in enumerate(chain):
            i = k + 2
            at = step(t, i, s, *(("ow", 0) if k == 0 else ("of", 18 * (k % 2 == 0))))
            now = me < 6 or i >= max(chain)
            exchange(t, 4 if now else 1)
            unpack(t, todo, "s" * UNPACK[t][me][k][0], now)
            got = wrap(i, *at, offsets=k + 1 < len(chain))
            unpack(t, todo, "v" * UNPACK[t][me][k][1], now)
        ts(R("oz"), got, unit, A.mult, R("pf"), A.add)
        unpack(t, todo, "sv" * 8)
        exchange(t)
        return got

    def serve(t):
        def some(o0, o1, planes):
            for b in planes:
                copy("sv"[b % 2], R("gb%d" % t, 64 * o0 + b, 64 * o1, 4), R("z", M * b, M * b + M + HALF), R("oz", o0, o1))

        def off(c0, c1):
            quant(R("gq%d" % t, c0, c1), R("gs%d" % t, c0, c1), R("gb%d" % t, 4 * c0, 4 * c1))
            send("g", "b", t, c0, c1)
        if me in HALVES:
            some(0, 10, range(4))
            some(10, 18, range(3))
            off(0, 144)
            some(10, 18, [3])
            off(144, C)
        else:
            some(0, 18, range(4))
            off(0, C)
        land("g", "b", t)

    def lists_out(got):
        name, row = PLAIN
        ts(R("opl"), got, unit, A.mult, float(zero), A.add)
        copy("s", R("pr"), R(name), R("opl"))
        for r in range(N):
            s = R("pr", 36 * r, 36 * r + 36)
            to, sem = ("dq", "pa") if r == me else ("dp", "p0")
            dma("y", sem, T[to][r, 0:96, :], T.pr[row:128:16, 36 * r:36 * r + 36], [s], [slot(to, r)])
        spread(lambda r: T.dp[r], T.dq[me], [slots("dp")], "pa")
        arrives("pa", N - 1, [slot("dq", r) for r in others])

    def take(t, k0, k1):
        zp, h = "zpb%d" % t, "hb%d" % t
        skip = 128 - 36 * (k1 - k0)
        for f in (0, 1):
            c0 = landing("b", 2 * k0 + f, t)[0] - skip
            for i in range(8):
                mm(i, *shift(i // 4, f, i % 4), R("lq%d" % t, c0, c0 + 128), R("ls%d" % t, c0, c0 + 128), f == 0, f == 1)
        for i in range(8):
            e, b = i // 4, i % 4
            for k in range(k0, k1):
                o = 36 * (k - k0) + skip
                copy("vs"[i % 2], R(zp, C * k + 144 * e + b, C * k + 144 * e + 144, 4), R("pb%d" % i, o, o + 36))
        for k in range(k0, k1):
            for a in range(4):
                o, s = R(h, C * a, C * a + C, 1, 32 * k, 32 * k + 32), R(zp, C * k, C * k + C, 1, 32 * a, 32 * a + 32)
                if k < 2:
                    move("ta%d" % t, o, s)
                else:
                    copy("vvsv"[a], o, s)

    def layer(t):
        for c in (0, 144):
            hq, hs = R("hq%d" % t, c, c + 144), R("hs%d" % t, c, c + 144)
            quant(hq, hs, R("hb%d" % t, 4 * c, 4 * c + 576))
            for b in range(4):
                mm(b + c // 36, R("wq", 128 * b, 128 * b + 128), R("wp", 128 * b, 128 * b + 128), hq, hs)
        for c in (0, 144):
            for b in range(4):
                out, src = R("x%d" % (t + 1), 4 * c + b, 4 * c + 576, 4), R("pb%d" % (b + c // 36), 0, 144)
                if b % 2 == 0:
                    op("s", lambda: g.scalar.activation(ap(out), ap(src), ACT.Relu, scale=0.03125), [src], [out])
                else:
                    ts(out, src, 0.0, A.max, 0.03125, A.mult)
            product(t + 1, c)

    dma("s", "ls", T.si[0:16, :], T.sc[:], [], [R("si", p1=16)])
    dma("y", "lx", ap(R("x0")), T.x[:], [], [R("x0")])
    iota(R("sg", 0, C), [[32, 9], [C, 2], [1, 16]], -HALF, 0)
    iota(R("sv", 0, C), [[1, C]], 0, 0)
    iota(R("rt"), [[C, 8], [1, 36]], 0, 0)
    iota(R("valm"), [[-64, 2], [0, 4], [-1, 16]], 0, 1)
    for k in range(4):
        fill(R("bi", k, k + 1), (16 + C * FRAC, 2 * C * (1 + FRAC), 4 * C * (1 + FRAC), 0.0)[k])
        fill(R("bj", k, k + 1), 36.0 * 2 ** k)
    fill(R("srow", C, 384, p1=32), 0.0)
    successors_out()
    fill(R("rb"), 0.0)
    dma("y", "lu", T.ub[:], T.u[:], [], [R("ub")])
    ts(R("sv", C, 2 * C), R("sv", 0, C), FRAC, A.mult)
    tt(R("st", 0, C), R("sg", 0, C), R("sv", C, 2 * C), A.add)
    dma("y", "nu", T.st[2:128:16, 0:C], T.rt[2:128:16, :], [R("rt")], [R("st", 0, C)])
    dma("y", "nu", T.bi[2:128:16, :], T.bj[2:128:16, :], [R("bj")], [R("bi")])
    dma("y", "lw", bits(R("wq")), T.wc[:], [], [R("wq")])
    dma("y", "lw", T.wp[:], T.ws[:], [], [R("wp")])

    for t in range(ROUNDS):
        last = t == ROUNDS - 1
        if t == 0:
            runs(t)
            parts(t)
            score(t)
            fill(R("gt"), 0.0)
            successors_in([me])
            grow()
            movers(0)
            successors_in(others)
        else:
            score(t)
            runs(t)
            quant(R("vq"), R("vs"), R("vb"))
            parts(t)
        score_rows(t)
        hop1(t)
        if t == 0:
            movers(1)
            iota(R("vale"), [[-32, 4], [256, 2], [-1, 16]], 0, 1)
            fill(R("ct", 4 * 516), 0.0)
            fill(R("pf", p1=64), float(HALF + zero))
            fill(R("pf", p0=64), float(zero))
            successor_offsets()
            dma("y", "p0", T.dp[:, 96:128, :], T.srow[0:N, C:384], [R("srow", C, 384, p1=N)], [slots("dp")])
        first_list(t)
        got = lists(t)
        serve(t)
        if last:
            lists_out(got)
        else:
            dma("y", "lv", T.vb[:], T.v[:], [], [R("vb")])
            strips(1)
        take(t, 0, 2)
        take(t, 2, 3)
        if last:
            dma("y", "out", T.pl[:], T.dq[:, 0:96, :], [slots("dq")], [])
        take(t, 3, 4)
        layer(t)

    xq, xs = R("xq%d" % ROUNDS), R("xs%d" % ROUNDS)
    for c in (0, 144):
        half = R(xq[0], c, c + 144)
        dma("y", "out", T.oc[:, 4 * c:4 * c + 576], bits(half), [half], [])
        if c:
            for k in range(4):
                dma("yyss"[k], "out", T.osc[4 * k:4 * k + 4, :], T[xs[0]][32 * k:32 * k + 4, :], [xs], [])
        copy("sv"[c // 144], R("yo", c, c + 144), R("pb%d" % (c // 36), 0, 144))
        dma("ys"[c // 144], "out", T.y[:, c:c + 144], T.yo[:, c:c + 144], [R("yo", c, c + 144)], [])
    for name in groups:
        wait("g", (name, None))
    for e in done:
        wait("g", (done[e]["sem"], done[e]["n"]))
